import numpy as np, ml_dtypes
CORES = [16,17,18,19,32,33,34,35]
N = 8
BF = ml_dtypes.bfloat16
S, A, L, M, R, D = 128, 32, 32, 2, 32, 16
def steps(nx, sy):
    g = np.arange(8); s = np.zeros(8, np.int64); place = np.zeros((N * L, 8), np.int64); cnt = np.zeros((N * L, 8), np.int64)
    for i in range(N * L):
        place[i] = sy[i // L, :, i % L].astype(np.int64) * S + s
        v = nx[i // L, g, place[i]].astype(np.int64)
        s = v % S; cnt[i] = v // S
    return place, cnt
def counts(rng, uneven=False):
    k = np.argsort(rng.random((N, 8, S, A)), -1)
    w = rng.integers(0, 2, k.shape) * M if uneven else rng.integers(0, M + 1, k.shape)
    return np.ascontiguousarray(np.where(k <= M, k, w).transpose(0, 1, 3, 2))
def perms(rng):
    return np.argsort(rng.random((N, 8, A, S)), -1)
def bounds(rng):
    e = np.zeros((8, N + 1), np.int64)
    e[:, 1:N] = np.arange(1, N) * R + rng.integers(-D, D + 1, (8, N - 1)); e[:, N] = N * R - rng.integers(0, D + 1, 8)
    e[0, N] = N * R - D; e[7, N] = N * R
    return e
def draw(rng, to, ct, e, burst=False):
    n = (e[:, 1:] - e[:, :-1])[:, :, None]
    k = (np.arange(L * M) - M * rng.integers(0, L, (8, N, 1))) % (L * M) if burst else np.argsort(rng.random((8, N, L * M)), -1)
    c = np.sum((k < n).reshape(8, N, L, M), axis=-1)
    g = np.arange(8); s = np.zeros(8, np.int64); sy = np.zeros((N, 8, L), np.int32)
    for i in range(N * L):
        q = i // L; ok = ct[q][g, :, s] == c[:, q, i % L][:, None]
        a = np.argmax(np.where(ok, rng.random((8, A)), -1.0), axis=1)
        sy[q, :, i % L] = a; s = to[q][g, a, s]
    return {"nx": (ct * S + to).reshape(N, 8, A * S).astype(np.int32), "em": rng.integers(0, 64 ** M, (N, 8, A * S)).astype(np.int32), "sy": sy}
def setup_inputs(rng):
    to = np.where(rng.random((N, 8, A, 1)) < 0.125, rng.integers(0, S, (N, 8, A, S)), perms(rng))
    return draw(rng, to, counts(rng), bounds(rng))
def setup_inputs_edge(rng):
    e = bounds(rng); g = np.arange(8)[:, None]; r = np.arange(1, N)[None, :]
    e[:, 1:N] = r * R + D * np.where(g % 2 == 0, 1 - 2 * ((r + g // 2) % 2), 1 - 2 * (g // 2 % 2)); e[:, N] = N * R - D * (np.arange(8) // 4)
    return draw(rng, perms(rng), counts(rng), e)
def setup_inputs_even(rng):
    e = bounds(rng); e[:] = np.arange(N + 1) * R
    return draw(rng, perms(rng), counts(rng), e)
def setup_inputs_merge(rng):
    kind = (np.argsort(rng.random((N, 8, A)), -1) % 4)[:, :, :, None]; h = (N, 8, A, 1); s = np.arange(S)
    one = np.where(rng.random(h) < 0.5, rng.integers(0, 2, h) * (S - 1), rng.integers(0, S, h))
    to = np.where(kind == 0, one, np.where(kind == 1, s, np.where(kind == 2, (s + 1) % S, rng.integers(0, S, (N, 8, A, S)))))
    return draw(rng, to, counts(rng), bounds(rng))
def setup_inputs_spread(rng):
    to = np.minimum(np.floor(S * rng.random((N, 8, A, S)) ** 6), S - 1).astype(np.int64)
    d = draw(rng, to, counts(rng, True), bounds(rng), True)
    h = (N, 8, A * S); d["em"] = (d["em"] >> np.where(rng.random(h) < 0.5, rng.integers(0, 6 * M, h), 0)).astype(np.int32)
    return d
def check_inputs(d):
    bad = []
    for k, top in (("nx", (M + 1) * S), ("em", 64 ** M), ("sy", A)):
        if d[k].min() < 0 or d[k].max() >= top: bad.append("range of " + k)
    if bad: return bad
    place, cnt = steps(d["nx"], d["sy"])
    off = np.add.accumulate(cnt, 0)[L - 1::L] - R * np.arange(1, N + 1)[:, None]
    if (np.abs(off) > D).any(): bad.append("running totals")
    if (off[-1] > 0).any(): bad.append("whole total")
    return bad
def reference(nx, em, sy):
    place, cnt = steps(nx, sy); g = np.broadcast_to(np.arange(8), (N * L, 8)); r = (np.arange(N * L) // L)[:, None]
    e = em[r, g, place].astype(np.int64); beg = np.add.accumulate(cnt, 0) - cnt
    z = np.full((8, N * R), -1, np.int64)
    for m in range(M):
        on = cnt > m
        z[g[on], beg[on] + m] = ((e >> (6 * m)) & 63)[on]
    return {"y": np.ascontiguousarray(z.reshape(8, N, R).transpose(1, 0, 2)).astype(np.float32)}

@@ -1,0 +1,435 @@
+from concourse.bass import DstId, RemoteDMATransfer
+from concourse.mybir import dt, AluOpType, AxisListType, ActivationFunctionType
+
+SL = 144
+_BUF = {
+    "int32": "PI:1 CI:8 SYI:2x2x2x4 X:2x128 XA:2x128 EM:2x128 EI0:2x128 EI1:2x128",
+    "uint16": "LST:192 LA:32 LB:16 LC:8 CUR:80 X4:2 POFF:16 OFP:8 OF2:6",
+    "float32": "CF:8 RI:256 IR:128 GC:128 J16:256 BR:192 TR:16 MG:4 MS:16 MGP:8 TB0:1 TBC:1 QO:1 LT8:1 CORR:1 SD0:256 SD:256 "
+               "MK:128 RST:128 TM:16 TP:1 QI:6 LSF:192 SCA:512 SCB:256 SCC:128 JK:16 ST:4 TA:3x128 GV:128 SCN:128 POS:8 "
+               "C4S:1 C4:1 BG0:1 BG:1 NPV:1 NOW:1 YG:96 Y1:32 Y2:32",
+    "bfloat16": "R:256 XR:128 BO:128 RB:8x128 ONE:128 IO1:64 TL:16 TRI:128 SYB:2x2x2x4 XT:2x128 XS:2x128 EB:2x2x128 "
+                "DB:2x2x128 SEL:2x4x8 LS:2x4x64 YB:16x64 T3:128 W3:1024 W2:1024 W1:1024 W0:1024 QM:512 HM:256 MW:512 "
+                "M6:128 PW:1152 EW:1024 FL:8 INC:8 OH:8x64 F:%d" % (6 * SL),
+}
+SCRATCH = {n: ("sbuf", [128] + [int(x) for x in d.split("x")], t)
+           for t, l in _BUF.items() for n, d in (w.split(":") for w in l.split())}
+for _n, _d in (("PSA", [512]), ("PSL", [64, 8]), ("PWA", [512]), ("PWB", [512]), ("PTT", [4, 128]), ("PE0", [512]),
+               ("PE1", [512]), ("PSO", [512])):
+    SCRATCH[_n] = ("psum", [128] + _d, "float32")
+SEMAPHORES = (["v", "s", "t", "q", "dsy", "dx", "dxs", "dem", "dy", "ls", "x4", "eo", "c4"]
+              + ["e1_%d" % j for j in range(4)] + ["en_%d" % j for j in range(4)] + ["ev_%d" % j for j in range(4)])
+NE = 8
+
+
+def rank_program(g, core, T, topo):
+    rank = T.rank_of(core)
+    if rank is None:
+        return
+    OP, ACT, AX = AluOpType, ActivationFunctionType, AxisListType
+    mine = [r for r, c in enumerate(T.cores) if topo.chip(c) == topo.chip(core)]
+    rest = [r for r in range(len(T.cores)) if r not in mine]
+    j = mine.index(rank)
+    first = mine[0] == 0
+    Q = {"v": g.vector, "s": g.scalar, "t": g.tensor, "q": g, "y": g.sync}
+    cnt = {"v": 0, "s": 0, "t": 0, "q": 0}
+    seen = {}
+    V, S, PE = g.vector, g.scalar, g.tensor
+
+    def need(e, *toks):
+        for sem, n in toks:
+            if seen.get((e, sem), 0) < n:
+                Q[e].wait_ge(T.sem[sem], n)
+                seen[(e, sem)] = n
+
+    def did(e, ins):
+        cnt[e] += 1
+        ins.then_inc(T.sem[e], 1)
+        return (e, cnt[e])
+
+    def ts(out, in0, s1, op0, s2=None, op1=None):
+        if op1 is None:
+            return did("v", V.tensor_scalar(out, in0, s1, None, op0))
+        return did("v", V.tensor_scalar(out, in0, s1, s2, op0, op1))
+
+    def tt(out, in0, in1, op):
+        return did("v", V.tensor_tensor(out, in0, in1, op))
+
+    def vcopy(out, in_):
+        return did("v", V.tensor_copy(out, in_))
+
+    def fill(ap, x):
+        return did("v", V.memset(ap, x))
+
+    def scopy(out, in_, **k):
+        return did("s", S.activation(out, in_, ACT.Copy, **k))
+
+    def mm(out, lhsT, rhs, start=True, stop=True):
+        return did("t", PE.matmul(out, lhsT, rhs, start, stop))
+
+    def iota(out, pattern, cm=0):
+        if cm:
+            return did("q", g.iota(out, pattern, 0, cm))
+        return did("q", g.iota(out, pattern, 0, cm, allow_small_or_imprecise_dtypes=True))
+
+    g.sync.dma_start(T.SYI[0:8], T.sy[:, :]).then_inc(T.sem.dsy, 16)
+    g.sync.dma_start(T.X[:, 0, :], T.nx[0:4, :]).then_inc(T.sem.dx, 16)
+    S.dma_start(T.X[:, 1, :], T.nx[4:8, :]).then_inc(T.sem.dxs, 16)
+    g.sync.dma_start(T.EM[:, 0, :], T.em[0:4, :]).then_inc(T.sem.dem, 16)
+    g.sync.dma_start(T.EM[:, 1, :], T.em[4:8, :]).then_inc(T.sem.dem, 16)
+    dsy, dx, dxs, dem = ("dsy", 16), ("dx", 16), ("dxs", 16), ("dem", 32)
+
+    k_pi = iota(T.PI[:], [[0, 1]], 1)
+    k_ri = iota(T.RI[0:8, :], [[1, 8], [0, 32]])
+    k_ir = iota(T.IR[:], [[1, 128]])
+    k_gc = iota(T.GC[:], [[1, 8], [0, 16]])
+    k_br = iota(T.BR[:], [[0, 6], [128, 4], [0, 8]])
+    k_j16 = iota(T.J16[:], [[0, 16], [1, 16]])
+    k_xr = iota(T.XR[0:1, :], [[1, 128]])
+    iota(T.TR[:, 0:8], [[1, 2], [2, 2], [4, 2]])
+    k_tr = iota(T.TR[:, 8:16], [[1, 2], [2, 2], [4, 2]])
+
+    c_ls0 = fill(T.LS[:], 0.0)
+    c_one = fill(T.ONE[:], 1.0)
+    need("v", k_pi)
+    ts(T.CI[:, 0:1], T.PI[:], 15, OP.bitwise_and)
+    ts(T.CI[:, 1:2], T.PI[:], 31, OP.bitwise_and)
+    ts(T.CI[:, 2:3], T.PI[:], 5, OP.arith_shift_right)
+    ts(T.CI[:, 3:4], T.PI[:], 4, OP.arith_shift_right)
+    a = vcopy(T.CI[:, 4:5], T.PI[:])
+    need("v", a)
+    c_cf = vcopy(T.CF[:, 0:5], T.CI[:, 0:5])
+    q_, a_, gt_, gp_, p_ = [T.CF[:, i:i + 1] for i in range(5)]
+    need("v", c_cf, k_ri)
+    c_r = ts(T.R[0:8, :], T.RI[0:8, :], T.CF[0:8, 4:5], OP.is_equal)
+    need("v", k_ir)
+    c_mg = ts(T.MG[:], T.IR[:, 0:4], gt_, OP.is_equal)
+    c_ms = ts(T.MS[:], T.IR[:, 0:16], q_, OP.is_equal)
+    need("v", k_gc)
+    c_bo = ts(T.BO[:], T.GC[:], gp_, OP.is_equal)
+    need("v", c_ms)
+    a = tt(T.TB0[:], T.MS[:, 1:2], T.MS[:, 3:4], OP.add)
+    c_qo = ts(T.QO[:], q_, 128.0, OP.mult, 1024.0, OP.min)
+    c_corr = ts(T.CORR[:], q_, 512.0, OP.mult, -7680.0, OP.add)
+    c_lt8 = ts(T.LT8[:], q_, 8.0, OP.is_lt)
+    need("v", a)
+    c_tb = ts(T.TBC[:], T.TB0[:], 128.0, OP.mult)
+    need("s", c_bo, c_ms)
+    for b in range(8):
+        c_rb = scopy(T.RB[:, b, :], T.BO[:], scale=T.MS[:, b:b + 1])
+
+    need("v", dsy)
+    for e in range(2):
+        for h in range(2):
+            c_syb = vcopy(T.SYB[0:8, e, :, h, :], T.SYI[0:8, h, :, e, :])
+    need("t", c_syb, c_r)
+    for t in range(2):
+        p_rep = mm(T.PSA[:, 32 * t:32 * t + 32], T.R[0:8, 128 * t:128 * t + 128], T.SYB[0:8])
+    need("v", dx, dxs)
+    a = ts(T.XA[:], T.X[:], 127, OP.bitwise_and)
+    need("v", p_rep)
+    for k in range(4):
+        c_sel = ts(T.SEL[:, :, k, :], T.PSA[:, k:64:4], a_, OP.is_equal)
+    need("v", a)
+    c_xt = vcopy(T.XT[:], T.XA[:])
+    need("v", c_sel, c_mg, c_ls0)
+    for gg in range(4):
+        c_ls = ts(T.LS[:, :, :, 16 * gg:16 * gg + 8], T.SEL[:], T.MG[:, gg:gg + 1], OP.mult)
+    need("t", c_ls, c_xt)
+    for t in range(2):
+        p_t3 = mm(T.PSA[64 * t:64 * t + 64, 128:256], T.LS[:, t, 3, :], T.XT[:, t, :])
+    need("s", c_xt, c_mg)
+    for gg in range(2):
+        s_yb = scopy(T.YB[:, :, 16 * gg:16 * gg + 16], T.XT[:], scale=T.MG[:, gg:gg + 1])
+    need("v", c_xt)
+    for gg in range(2, 4):
+        c_yb = ts(T.YB[:, :, 16 * gg:16 * gg + 16], T.XT[:], T.MG[:, gg:gg + 1], OP.mult)
+    need("v", p_t3, c_tb)
+    c_t3 = ts(T.T3[:], T.PSA[:, 128:256], T.TBC[:], OP.add)
+    s_xs = scopy(T.XS[:], T.XT[:], scale=1.0 / 512.0)
+    need("t", c_t3, c_rb)
+    for b in range(4):
+        p_wa = mm(T.PWA[:, 128 * b:128 * b + 128], T.RB[:, b, :], T.T3[:])
+    for b in range(4):
+        p_wb = mm(T.PWB[:, 128 * b:128 * b + 128], T.RB[:, 4 + b, :], T.T3[:])
+    need("t", c_yb, s_yb, c_sel)
+    for t in range(2):
+        for c in range(8):
+            p_l = mm(T.PSL[64 * t:64 * t + 64, 0:24, c], T.YB[:, 8 * t + c, :], T.SEL[:, t, 0:3, :])
+    need("t", s_xs, k_xr, c_one)
+    for t in range(2):
+        for k in range(3):
+            mm(T.PTT[64 * t:64 * t + 64, k, :], T.ONE[0:1, 0:64], T.XR[0:1, :], True, False)
+            p_tt = mm(T.PTT[64 * t:64 * t + 64, k, :], T.LS[:, t, k, :], T.XS[:, t, :], False, True)
+    need("v", p_wa)
+    c_w = vcopy(T.W3[:, 0:512], T.PWA[:])
+    need("s", p_wb)
+    s_w = scopy(T.W3[:, 512:1024], T.PWB[:])
+    need("v", p_l, k_br)
+    a = tt(T.LSF[:], T.PSL[:, 0:24, :], T.BR[:], OP.add)
+    need("v", k_j16)
+    b = ts(T.SD0[:], T.J16[:], q_, OP.is_equal, -1048576.0, OP.mult)
+    need("v", a)
+    c_l = vcopy(T.LST[:], T.LSF[:])
+
+    src = T.W3
+    for k, dst in ((2, T.W2), (1, T.W1), (0, T.W0)):
+        need("v", c_w, c_l)
+        c_w = vcopy(dst[:, 0:512], src[:, 0:512].indirect(T.LST[:, 64 * k:64 * k + 32]))
+        if k == 2:
+            need("v", b)
+            c_sd = ts(T.SD[:], T.SD0[:], 512.0, OP.add)
+        need("s", s_w, c_l)
+        s_w = scopy(dst[:, 512:1024], src[:, 512:1024].indirect(T.LST[:, 64 * k + 32:64 * k + 64]))
+        src = dst
+
+    def scan(out, in_, n):
+        return did("v", V.tensor_tensor_scan(out, T.SD[:, 0:n], in_, 0.0, OP.add, OP.max))
+    need("v", c_w, c_sd)
+    x1 = scan(T.SCA[:, 256:512], T.W0[:, 256:512], 256)
+    x0 = scan(T.SCA[:, 0:256], T.W0[:, 0:256], 256)
+    need("v", x1)
+    l1 = ts(T.LA[:, 16:32], T.SCA[:, 271:512:16], T.CORR[:], OP.add)
+    need("v", x0)
+    l0 = ts(T.LA[:, 0:16], T.SCA[:, 15:256:16], T.CORR[:], OP.add)
+    need("v", l0, s_w)
+    c_q = vcopy(T.QM[:, 0:256], T.W0[:, 512:768].indirect(T.LA[:, 0:16]))
+    need("s", l1, s_w)
+    s_q = scopy(T.QM[:, 256:512], T.W0[:, 768:1024].indirect(T.LA[:, 16:32]))
+    need("v", c_q)
+    x0 = scan(T.SCB[:], T.QM[:, 0:256], 256)
+    need("v", x0)
+    c_lb = ts(T.LB[:], T.SCB[:, 15:256:16], T.CORR[:], OP.add)
+    need("v", c_lb, s_q)
+    c_h = vcopy(T.HM[:, 0:128], T.QM[:, 256:384].indirect(T.LB[:, 0:8]))
+    need("s", c_lb, s_q)
+    s_h = scopy(T.HM[:, 128:256], T.QM[:, 384:512].indirect(T.LB[:, 8:16]))
+    need("v", c_h)
+    x0 = scan(T.SCC[:], T.HM[:, 0:128], 128)
+    need("v", x0)
+    c_lc = ts(T.LC[:], T.SCC[:, 15:128:16], T.CORR[:], OP.add)
+    peers = [i for i in range(len(mine)) if i != j and (first or i > j)]
+    if peers:
+        need("v", c_lc, s_h)
+        c_m = vcopy(T.MW[:, 128 * j:128 * j + 128], T.HM[:, 128:256].indirect(T.LC[:]))
+    sent = [0]
+
+    def send(ranks, dst, src_, sem):
+        cores = [T.cores[r] for r in ranks]
+        es = [e for e in topo.engines(core, cores[0]) if all(e in topo.engines(core, c) for c in cores)][:NE]
+        ids = [DstId(rid=topo.addr(c)[0], pnc=topo.addr(c)[1]) for c in cores]
+        g.remote_dma_fused([RemoteDMATransfer(dst_ids=ids, dma_engine_mask=sum(1 << e for e in es), remote_sem=T.sem[sem],
+                                              srcs=[src_], dsts=[dst for _ in cores])], local_sem=T.sem.ls)
+        sent[0] += len(es)
+    if peers:
+        need("q", c_m)
+        send([mine[i] for i in peers], T.MW[:, 128 * j:128 * j + 128], T.MW[:, 128 * j:128 * j + 128], "e1_%d" % j)
+
+    def region(s):
+        return T.PW[:, 128 * s:128 * s + 128]
+    ms = [T.MS[:, s:s + 1] for s in range(8)]
+    s_m6 = scopy(T.M6[:], T.W0[:, 384:512].indirect(T.LB[:, 8:16]))
+    scopy(region(6), T.W0[:, 256:384].indirect(T.LB[:, 0:8]), scale=ms[6])
+    need("s", c_lc)
+    s_p = scopy(region(3), T.QM[:, 128:256].indirect(T.LC[:]), scale=ms[3])
+    ts(region(0), T.IR[:], ms[0], OP.mult)
+    fill(region(8), 0.0)
+    ts(region(4), T.W0[:, 0:128], ms[4], OP.mult)
+    ts(region(2), T.QM[:, 0:128], ms[2], OP.mult)
+    ts(region(1), T.HM[:, 0:128], ms[1], OP.mult)
+    need("v", c_lc)
+    ts(region(5), T.W0[:, 128:256].indirect(T.LC[:]), -128.0, OP.add, ms[5], OP.mult)
+    need("v", s_m6)
+    c_p = ts(region(7), T.M6[:].indirect(T.LC[:]), -128.0, OP.add, ms[7], OP.mult)
+    need("v", dem)
+    a = ts(T.EI0[:], T.EM[:], 63, OP.bitwise_and)
+    b = ts(T.EI1[:], T.EM[:], 6, OP.arith_shift_right)
+    ts(T.DB[:, :, 0, :], T.X[:], 128.0, OP.is_lt, -128.0, OP.mult)
+    ts(T.DB[:, :, 1, :], T.X[:], 256.0, OP.is_lt, -128.0, OP.mult)
+    need("v", a)
+    vcopy(T.EB[:, :, 0, :], T.EI0[:])
+    need("v", b)
+    c_eb = vcopy(T.EB[:, :, 1, :], T.EI1[:])
+    need("t", c_eb)
+    for k in range(4):
+        bank = T.PE0 if k < 2 else T.PE1
+        for t in range(2):
+            o = bank[64 * t:64 * t + 64, 256 * (k % 2):256 * (k % 2) + 256]
+            mm(o, T.LS[:, t, k, :], T.EB[:, t], True, False)
+            p_e = mm(o, T.LS[:, t, k, :], T.DB[:, t], False, True)
+        if k % 2:
+            need("s", p_e)
+            s_ew = did("s", S.activation(T.EW[:, 256 * (k - 1):256 * (k - 1) + 512], bank[:], ACT.Relu, bias=1.0))
+    own = SL * (1 + j)
+    need("v", c_lt8)
+    c_mk = ts(T.MK[:], T.J16[:, 0:128], q_, OP.is_equal, T.LT8[:], OP.mult)
+    c_rst = ts(T.RST[:], T.J16[:, 0:128], 0.0, OP.not_equal)
+    c_io1 = ts(T.IO1[:], T.IR[:, 0:64], 1.0, OP.add)
+    ts(T.MGP[:], T.IR[:, 0:8], gp_, OP.is_equal)
+    need("v", k_tr)
+    a = tt(T.TM[:], T.MS[:], T.TR[:], OP.mult)
+    fill(T.F[:, own:own + 48], -1.0)
+    fill(T.F[:, own + 112:own + 128], -1.0)
+    c_f = fill(T.F[:, own + 128:own + SL], 0.0)
+    need("v", a)
+    a = did("v", V.tensor_reduce(T.TP[:], T.TM[:], AX.X, OP.add))
+    lists = [(1 + j, "own")]
+    if rank > 0:
+        lists.append((j, "prev"))
+    if rank + 1 < len(T.cores):
+        lists.append((2 + j, "next"))
+    w0 = min(x for x, _ in lists)
+    w1 = max(x for x, _ in lists)
+    for i, (x, _) in enumerate(lists):
+        c_qi = ts(T.QI[:, 2 * i:2 * i + 2], T.IR[:, 0:17:16], q_, OP.add, float(SL * (x - w0) + 48 + 32 * rank), OP.add)
+    need("v", a)
+    c_tl = ts(T.TL[:], T.TR[:], T.TP[:], OP.is_gt)
+    need("s", c_tl)
+    for gg in range(8):
+        s_tri = scopy(T.TRI[:, 16 * gg:16 * gg + 16], T.TL[:], scale=T.MGP[:, gg:gg + 1])
+
+    def look(i, off):
+        if i != j:
+            need("v", ("e1_%d" % i, NE))
+        return T.MW[:, 128 * i:128 * i + 128].indirect(off)
+    if first:
+        c = None
+        for i in range(len(mine)):
+            if i == 0:
+                need("v", c_m if j == 0 else ("e1_0", NE))
+                c = vcopy(T.CUR[:, 0:1], T.MW[:, 0:1])
+            else:
+                need("v", c, c_m)
+                c = vcopy(T.CUR[:, 16 * i:16 * i + 16], look(i, T.CUR[:, 16 * (i - 1):16 * (i - 1) + 1]))
+        need("q", c)
+        send([rest[j]], T.X4[:], T.CUR[:, 48:50], "x4")
+        if j == 0:
+            c_po = vcopy(T.POFF[:, 0:1], T.QO[:])
+        else:
+            c_po = ts(T.POFF[:, 0:1], T.CUR[:, 16 * (j - 1):16 * (j - 1) + 1], T.QO[:], OP.add)
+    else:
+        need("v", ("x4", NE))
+        off = T.X4[:, 0:1]
+        if j == 0:
+            c_po = ts(T.POFF[:, 0:1], off, T.QO[:], OP.add)
+        for i in range(j):
+            if i + 1 < j:
+                c = vcopy(T.CUR[:, 16 * i:16 * i + 16], look(i, off))
+                need("v", c)
+                off = T.CUR[:, 16 * i:16 * i + 1]
+            else:
+                c_po = ts(T.POFF[:], look(i, off), T.QO[:], OP.add)
+    need("s", c_po, c_p, s_p)
+    st = scopy(T.JK[:], T.PW[:].indirect(T.POFF[:, 0:1]), accum_out=T.ST[:, 0:1])
+    need("v", p_tt)
+    for k in range(4):
+        need("v", st)
+        col = T.ST[:, k:k + 1]
+        if k < 3:
+            a = ts(T.TA[:, k, :], T.PTT[:, k, :], col, OP.subtract, 512.0, OP.mult)
+        for m in range(2):
+            c_of = ts(T.OFP[:, 2 * k + m:2 * k + m + 1], col, float(128 * (2 * k + m)), OP.add)
+        if k < 3:
+            need("v", a)
+            st = did("v", V.tensor_reduce(T.ST[:, k + 1:k + 2], T.TA[:, k, :], AX.X, OP.min, apply_absolute_value=True))
+    need("v", c_of, s_ew, c_mk)
+    a = tt(T.GV[:], T.EW[:].indirect(T.OFP[:]), T.MK[:], OP.mult)
+    need("v", a, c_rst)
+    a = did("v", V.tensor_tensor_scan(T.SCN[:], T.RST[:], T.GV[:], 0.0, OP.mult, OP.add))
+    need("v", a)
+    a = ts(T.FL[:], T.SCN[:, 15:128:16], 0.0, OP.is_gt)
+    need("v", a)
+    c_inc = did("v", V.tensor_tensor_scan(T.INC[:], T.ONE[:, 0:8], T.FL[:], 0.0, OP.mult, OP.add))
+    need("t", c_inc, s_tri)
+    mm(T.PSO[:, 0:1], T.TRI[:], T.INC[:, 7:8])
+    p_n = mm(T.PSO[:, 1:2], T.BO[:], T.INC[:, 7:8])
+    need("v", p_n, c_inc)
+    a = ts(T.POS[:], T.INC[:], T.PSO[:, 0:1], OP.add)
+    need("v", c_f)
+    vcopy(T.NOW[:], T.PSO[:, 1:2])
+    c_n = vcopy(T.F[:, own + 128:own + 129], T.PSO[:, 1:2])
+    need("v", a, c_io1)
+    for i in range(8):
+        a = ts(T.OH[:, i, :], T.IO1[:], T.POS[:, i:i + 1], OP.is_equal, T.SCN[:, 16 * i + 15:16 * i + 16], OP.mult)
+        need("t", a)
+        p_a = mm(T.PSA[:, 256:320], T.BO[:], T.OH[:, i, :], i == 0, i == 7)
+    need("v", p_a)
+    c_a = ts(T.F[:, own + 48:own + 112], T.PSA[:, 256:320], -1.0, OP.add)
+
+    def part(x, lo, hi):
+        return T.F[:, SL * x + lo:SL * x + hi]
+    if first:
+        need("q", c_n)
+        send([r for r in mine if r != rank], part(1 + j, 128, SL), part(1 + j, 128, SL), "en_%d" % j)
+        need("q", c_a)
+        if j + 1 == len(mine):
+            send([rank + 1], part(0, 0, SL), part(1 + j, 0, SL), "eo")
+        near = [r for r in mine if abs(r - rank) == 1]
+        send(near, part(1 + j, 0, 128), part(1 + j, 0, 128), "ev_%d" % j)
+        for i in range(len(mine)):
+            if i != j:
+                need("v", ("en_%d" % i, NE))
+        need("v", c_n)
+        x0 = SL + 128
+        c_4 = did("v", V.tensor_reduce(T.C4S[:], T.F[:, x0:x0 + 3 * SL + 1:SL], AX.X, OP.add))
+        need("q", c_4)
+        send([rest[j]], T.C4[:], T.C4S[:], "c4")
+    else:
+        need("q", c_a, c_n)
+        near = [r for r in mine if r > rank or r == rank - 1]
+        send(near, part(1 + j, 0, SL), part(1 + j, 0, SL), "ev_%d" % j)
+        if j == 0:
+            send([rank - 1], part(1 + len(mine), 0, 128), part(1, 0, 128), "eo")
+
+    if first:
+        got = [i for i in range(len(mine)) if abs(i - j) == 1]
+    else:
+        got = [i for i in range(len(mine)) if i < j or i == j + 1]
+    for i in got:
+        need("v", ("ev_%d" % i, NE))
+    if (first and j + 1 == len(mine)) or (not first and j == 0):
+        need("v", ("eo", NE))
+    x0 = SL + 128
+    beg = 0.0
+    if rank > 0:
+        c_np = vcopy(T.NPV[:], part(j, 128, 129))
+        need("v", c_np)
+    if j == 1:
+        beg = T.NPV[:]
+    elif j > 1:
+        a = did("v", V.tensor_reduce(T.BG0[:], T.F[:, x0:x0 + SL * (j - 1) + 1:SL], AX.X, OP.add))
+        need("v", a)
+        beg = T.BG0[:]
+    if not first:
+        need("v", ("c4", NE))
+        if j == 0:
+            beg = T.C4[:]
+        else:
+            a = tt(T.BG[:], T.C4[:], beg, OP.add)
+            need("v", a)
+            beg = T.BG[:]
+    need("v", c_qi, c_a, c_n)
+    for i, (x, what) in enumerate(lists):
+        o, q2 = T.OF2[:, 2 * i:2 * i + 2], T.QI[:, 2 * i:2 * i + 2]
+        if what == "own":
+            a = ts(o, q2, beg, OP.subtract)
+        elif what == "prev":
+            a = ts(o, q2, beg, OP.subtract, T.NPV[:], OP.add)
+        else:
+            a = ts(o, q2, beg, OP.subtract, T.NOW[:], OP.subtract)
+    n = len(lists)
+    need("v", a)
+    a = vcopy(T.YG[:, 0:32 * n], T.F[:, SL * w0:SL * w1 + 128].indirect(T.OF2[:, 0:2 * n]))
+    need("v", a)
+    out = T.Y1
+    a = tt(T.Y1[:], T.YG[:, 0:32], T.YG[:, 32:64], OP.max)
+    if n == 3:
+        need("v", a)
+        out = T.Y2
+        a = tt(T.Y2[:], T.Y1[:], T.YG[:, 64:96], OP.max)
+    need("y", a)
+    g.sync.dma_start(T.y[:, :], out[0:128:16, :]).then_inc(T.sem.dy, 16)
+    need("y", ("dy", 16))
+    for e in ("v", "s", "t", "q"):
+        need("q", (e, cnt[e]))
+    need("q", ("ls", sent[0]))

@@ -4,22 +4,21 @@ from concourse.mybir import dt, AluOpType, AxisListType, ActivationFunctionType
 SL = 144
 _BUF = {
     "int32": "PI:1 CI:8 SYI:2x2x2x4 X:2x128 XA:2x128 EM:2x128 EI0:2x128 EI1:2x128",
-    "uint16": "LST:192 LA:32 LB:16 LC:8 CUR:80 X4:2 POFF:16 OFP:8 OF2:6",
-    "float32": "CF:8 RI:256 IR:128 GC:128 J16:256 BR:192 TR:16 MG:4 MS:16 MGP:8 TB0:1 TBC:1 QO:1 LT8:1 CORR:1 SD0:256 SD:256 "
-               "MK:128 RST:128 TM:16 TP:1 QI:6 LSF:192 SCA:512 SCB:256 SCC:128 JK:16 ST:4 TA:3x128 GV:128 SCN:128 POS:8 "
-               "C4S:1 C4:1 BG0:1 BG:1 NPV:1 NOW:1 YG:96 Y1:32 Y2:32",
+    "uint16": "LST:192 LA:32 LB:16 LC:8 LL:64 POFF:16 X4:16 OFP:8 OF2:6",
+    "float32": "CF:8 RI:256 IR:128 GC:128 J16:128 BR:192 TR:16 MG:4 MS:16 MGP:8 QO:1 LT8:1 Q1:1 CORR:1 SD0:128 SD1:128 "
+               "TM:16 TP:1 QI:6 LSF:192 JK:16 ST:4 TA:3x128 C4:1 BG0:1 BG:1 NPV:1 NOW:1 YG:96 Y1:32 Y2:32",
     "bfloat16": "R:256 XR:128 BO:128 RB:8x128 ONE:128 IO1:64 TL:16 TRI:128 SYB:2x2x2x4 XT:2x128 XS:2x128 EB:2x2x128 "
-                "DB:2x2x128 SEL:2x4x8 LS:2x4x64 YB:16x64 T3:128 W3:1024 W2:1024 W1:1024 W0:1024 QM:512 HM:256 MW:512 "
-                "M6:128 PW:1152 EW:1024 FL:8 INC:8 OH:8x64 F:%d" % (6 * SL),
+                "DB:2x2x128 SEL:2x4x8 LS:2x4x64 YB:16x64 T3:128 W3:1024 W2:1024 W1:1024 W0:1024 QM:512 HM:256 MM:128 "
+                "SD:128 SCA:512 SCB:256 SCC:128 SCM:128 FB:896 M6:128 PW:1152 EW:1024 MK:128 RST:128 GV:128 SCN:128 "
+                "FL:8 INC:8 POS:8 OH:8x64 NB:64 F:%d" % (6 * SL),
 }
 SCRATCH = {n: ("sbuf", [128] + [int(x) for x in d.split("x")], t)
            for t, l in _BUF.items() for n, d in (w.split(":") for w in l.split())}
 for _n, _d in (("PSA", [512]), ("PSL", [64, 8]), ("PWA", [512]), ("PWB", [512]), ("PTT", [4, 128]), ("PE0", [512]),
                ("PE1", [512]), ("PSO", [512])):
     SCRATCH[_n] = ("psum", [128] + _d, "float32")
-SEMAPHORES = (["v", "s", "t", "q", "dsy", "dx", "dxs", "dem", "dy", "ls", "x4", "eo", "c4"]
-              + ["e1_%d" % j for j in range(4)] + ["en_%d" % j for j in range(4)] + ["ev_%d" % j for j in range(4)])
-NE = 8
+SEMAPHORES = (["v", "s", "t", "q", "dsy", "dx", "dxs", "dem", "dy", "ls"]
+              + [p + "_%d" % j for p in ("e1", "en", "ev") for j in range(8)])
 
 
 def rank_program(g, core, T, topo):
@@ -27,8 +26,8 @@ def rank_program(g, core, T, topo):
     if rank is None:
         return
     OP, ACT, AX = AluOpType, ActivationFunctionType, AxisListType
+    NR = len(T.cores)
     mine = [r for r, c in enumerate(T.cores) if topo.chip(c) == topo.chip(core)]
-    rest = [r for r in range(len(T.cores)) if r not in mine]
     j = mine.index(rank)
     first = mine[0] == 0
     Q = {"v": g.vector, "s": g.scalar, "t": g.tensor, "q": g, "y": g.sync}
@@ -72,6 +71,44 @@ def rank_program(g, core, T, topo):
             return did("q", g.iota(out, pattern, 0, cm))
         return did("q", g.iota(out, pattern, 0, cm, allow_small_or_imprecise_dtypes=True))
 
+    def same(r, r2):
+        return topo.chip(T.cores[r]) == topo.chip(T.cores[r2])
+
+    def plan(r, dsts):
+        near, far = [d for d in dsts if same(r, d)], [d for d in dsts if not same(r, d)]
+        p = []
+        if near:
+            es = topo.engines(T.cores[r], T.cores[near[0]])
+            if far or r + 1 == NR:
+                other = [d for d in range(NR) if not same(r, d)][0]
+                es = [e for e in es if e not in topo.engines(T.cores[r], T.cores[other])]
+            p.append((near, es))
+        if far:
+            p.append((far, topo.engines(T.cores[r], T.cores[far[0]])))
+        return p
+
+    def later(r):
+        return list(range(NR - 1, r, -1))
+
+    def e2(r):
+        d = [x for x in range(NR) if abs(x - r) == 1]
+        return d if same(r, 0) else d + [x for x in later(r) if x not in d]
+
+    def arrive(kind, r):
+        dsts = e2(r) if kind == "ev" else later(r)
+        return ("%s_%d" % (kind, r), [len(es) for ds, es in plan(r, dsts) if rank in ds][0])
+    sent = [0]
+
+    def send(kind, dsts, src_, where):
+        trs = []
+        for ds, es in plan(rank, dsts):
+            adr = [topo.addr(T.cores[d]) for d in ds]
+            trs.append(RemoteDMATransfer(dst_ids=[DstId(rid=x[0], pnc=x[1]) for x in adr],
+                                         dma_engine_mask=sum(1 << e for e in es),
+                                         remote_sem=T.sem["%s_%d" % (kind, rank)], srcs=[src_], dsts=[where(d) for d in ds]))
+            sent[0] += len(es)
+        g.remote_dma_fused(trs, local_sem=T.sem.ls)
+
     g.sync.dma_start(T.SYI[0:8], T.sy[:, :]).then_inc(T.sem.dsy, 16)
     g.sync.dma_start(T.X[:, 0, :], T.nx[0:4, :]).then_inc(T.sem.dx, 16)
     S.dma_start(T.X[:, 1, :], T.nx[4:8, :]).then_inc(T.sem.dxs, 16)
@@ -83,11 +120,11 @@ def rank_program(g, core, T, topo):
     k_ri = iota(T.RI[0:8, :], [[1, 8], [0, 32]])
     k_ir = iota(T.IR[:], [[1, 128]])
     k_gc = iota(T.GC[:], [[1, 8], [0, 16]])
-    k_br = iota(T.BR[:], [[0, 6], [128, 4], [0, 8]])
-    k_j16 = iota(T.J16[:], [[0, 16], [1, 16]])
-    k_xr = iota(T.XR[0:1, :], [[1, 128]])
     iota(T.TR[:, 0:8], [[1, 2], [2, 2], [4, 2]])
     k_tr = iota(T.TR[:, 8:16], [[1, 2], [2, 2], [4, 2]])
+    k_j16 = iota(T.J16[:], [[0, 8], [1, 16]])
+    k_br = iota(T.BR[:], [[0, 6], [128, 4], [0, 8]])
+    k_xr = iota(T.XR[0:1, :], [[1, 128]])
 
     c_ls0 = fill(T.LS[:], 0.0)
     c_one = fill(T.ONE[:], 1.0)
@@ -107,13 +144,11 @@ def rank_program(g, core, T, topo):
     c_ms = ts(T.MS[:], T.IR[:, 0:16], q_, OP.is_equal)
     need("v", k_gc)
     c_bo = ts(T.BO[:], T.GC[:], gp_, OP.is_equal)
-    need("v", c_ms)
-    a = tt(T.TB0[:], T.MS[:, 1:2], T.MS[:, 3:4], OP.add)
-    c_qo = ts(T.QO[:], q_, 128.0, OP.mult, 1024.0, OP.min)
-    c_corr = ts(T.CORR[:], q_, 512.0, OP.mult, -7680.0, OP.add)
+    ts(T.QO[:], q_, 128.0, OP.mult, 1024.0, OP.min)
+    ts(T.CORR[:], q_, 15.0, OP.is_lt, -128.0, OP.mult)
+    ts(T.Q1[:], q_, 1.0, OP.add)
+    ts(T.MGP[:], T.IR[:, 0:8], gp_, OP.is_equal)
     c_lt8 = ts(T.LT8[:], q_, 8.0, OP.is_lt)
-    need("v", a)
-    c_tb = ts(T.TBC[:], T.TB0[:], 128.0, OP.mult)
     need("s", c_bo, c_ms)
     for b in range(8):
         c_rb = scopy(T.RB[:, b, :], T.BO[:], scale=T.MS[:, b:b + 1])
@@ -144,31 +179,43 @@ def rank_program(g, core, T, topo):
     need("v", c_xt)
     for gg in range(2, 4):
         c_yb = ts(T.YB[:, :, 16 * gg:16 * gg + 16], T.XT[:], T.MG[:, gg:gg + 1], OP.mult)
-    need("v", p_t3, c_tb)
-    c_t3 = ts(T.T3[:], T.PSA[:, 128:256], T.TBC[:], OP.add)
+    need("v", p_t3)
+    c_t3 = vcopy(T.T3[:], T.PSA[:, 128:256])
     s_xs = scopy(T.XS[:], T.XT[:], scale=1.0 / 512.0)
     need("t", c_t3, c_rb)
     for b in range(4):
         p_wa = mm(T.PWA[:, 128 * b:128 * b + 128], T.RB[:, b, :], T.T3[:])
-    for b in range(4):
-        p_wb = mm(T.PWB[:, 128 * b:128 * b + 128], T.RB[:, 4 + b, :], T.T3[:])
     need("t", c_yb, s_yb, c_sel)
     for t in range(2):
         for c in range(8):
             p_l = mm(T.PSL[64 * t:64 * t + 64, 0:24, c], T.YB[:, 8 * t + c, :], T.SEL[:, t, 0:3, :])
+    for b in range(4):
+        p_wb = mm(T.PWB[:, 128 * b:128 * b + 128], T.RB[:, 4 + b, :], T.T3[:])
     need("t", s_xs, k_xr, c_one)
     for t in range(2):
         for k in range(3):
             mm(T.PTT[64 * t:64 * t + 64, k, :], T.ONE[0:1, 0:64], T.XR[0:1, :], True, False)
             p_tt = mm(T.PTT[64 * t:64 * t + 64, k, :], T.LS[:, t, k, :], T.XS[:, t, :], False, True)
+    need("v", k_tr)
+    a = tt(T.TM[:], T.MS[:], T.TR[:], OP.mult)
+    need("v", k_j16)
+    x0 = ts(T.SD0[:], T.J16[:], q_, OP.is_equal, -65536.0, OP.mult)
+    need("v", a)
+    a = did("v", V.tensor_reduce(T.TP[:], T.TM[:], AX.X, OP.add))
+    x1 = ts(T.SD1[:], T.J16[:], T.Q1[:], OP.is_equal, 128.0, OP.mult)
+    need("v", a)
+    c_tl = ts(T.TL[:], T.TR[:], T.TP[:], OP.is_gt)
+    need("s", c_tl)
+    for gg in range(8):
+        s_tri = scopy(T.TRI[:, 16 * gg:16 * gg + 16], T.TL[:], scale=T.MGP[:, gg:gg + 1])
     need("v", p_wa)
     c_w = vcopy(T.W3[:, 0:512], T.PWA[:])
     need("s", p_wb)
     s_w = scopy(T.W3[:, 512:1024], T.PWB[:])
+    need("v", x0, x1)
+    c_sd = tt(T.SD[:], T.SD0[:], T.SD1[:], OP.add)
     need("v", p_l, k_br)
     a = tt(T.LSF[:], T.PSL[:, 0:24, :], T.BR[:], OP.add)
-    need("v", k_j16)
-    b = ts(T.SD0[:], T.J16[:], q_, OP.is_equal, -1048576.0, OP.mult)
     need("v", a)
     c_l = vcopy(T.LST[:], T.LSF[:])
 
@@ -176,54 +223,44 @@ def rank_program(g, core, T, topo):
     for k, dst in ((2, T.W2), (1, T.W1), (0, T.W0)):
         need("v", c_w, c_l)
         c_w = vcopy(dst[:, 0:512], src[:, 0:512].indirect(T.LST[:, 64 * k:64 * k + 32]))
-        if k == 2:
-            need("v", b)
-            c_sd = ts(T.SD[:], T.SD0[:], 512.0, OP.add)
         need("s", s_w, c_l)
         s_w = scopy(dst[:, 512:1024], src[:, 512:1024].indirect(T.LST[:, 64 * k + 32:64 * k + 64]))
         src = dst
 
-    def scan(out, in_, n):
-        return did("v", V.tensor_tensor_scan(out, T.SD[:, 0:n], in_, 0.0, OP.add, OP.max))
+    def to_lists(lst, sc, win, slots):
+        for s in slots:
+            x = did("v", V.tensor_tensor_scan(sc[:, 128 * s:128 * s + 128], T.SD[:], win[:, 128 * s:128 * s + 128], 0.0,
+                                              OP.add, OP.max))
+        need("v", x)
+        s, n = slots[0], len(slots)
+        return ts(lst[:, 8 * s:8 * s + 8 * n], sc[:, 128 * s + 15:128 * (s + n):16], T.CORR[:], OP.add)
     need("v", c_w, c_sd)
-    x1 = scan(T.SCA[:, 256:512], T.W0[:, 256:512], 256)
-    x0 = scan(T.SCA[:, 0:256], T.W0[:, 0:256], 256)
-    need("v", x1)
-    l1 = ts(T.LA[:, 16:32], T.SCA[:, 271:512:16], T.CORR[:], OP.add)
-    need("v", x0)
-    l0 = ts(T.LA[:, 0:16], T.SCA[:, 15:256:16], T.CORR[:], OP.add)
+    l1 = to_lists(T.LA, T.SCA, T.W0, [2, 3])
+    l0 = to_lists(T.LA, T.SCA, T.W0, [0, 1])
     need("v", l0, s_w)
-    c_q = vcopy(T.QM[:, 0:256], T.W0[:, 512:768].indirect(T.LA[:, 0:16]))
     need("s", l1, s_w)
-    s_q = scopy(T.QM[:, 256:512], T.W0[:, 768:1024].indirect(T.LA[:, 16:32]))
+    for s in range(2):
+        c_q = vcopy(T.QM[:, 128 * s:128 * s + 128], T.W0[:, 512 + 128 * s:640 + 128 * s].indirect(T.LA[:, 8 * s:8 * s + 8]))
+    for s in range(2, 4):
+        s_q = scopy(T.QM[:, 128 * s:128 * s + 128], T.W0[:, 512 + 128 * s:640 + 128 * s].indirect(T.LA[:, 8 * s:8 * s + 8]))
     need("v", c_q)
-    x0 = scan(T.SCB[:], T.QM[:, 0:256], 256)
-    need("v", x0)
-    c_lb = ts(T.LB[:], T.SCB[:, 15:256:16], T.CORR[:], OP.add)
+    c_lb = to_lists(T.LB, T.SCB, T.QM, [0, 1])
     need("v", c_lb, s_q)
     c_h = vcopy(T.HM[:, 0:128], T.QM[:, 256:384].indirect(T.LB[:, 0:8]))
     need("s", c_lb, s_q)
     s_h = scopy(T.HM[:, 128:256], T.QM[:, 384:512].indirect(T.LB[:, 8:16]))
     need("v", c_h)
-    x0 = scan(T.SCC[:], T.HM[:, 0:128], 128)
-    need("v", x0)
-    c_lc = ts(T.LC[:], T.SCC[:, 15:128:16], T.CORR[:], OP.add)
-    peers = [i for i in range(len(mine)) if i != j and (first or i > j)]
-    if peers:
-        need("v", c_lc, s_h)
-        c_m = vcopy(T.MW[:, 128 * j:128 * j + 128], T.HM[:, 128:256].indirect(T.LC[:]))
-    sent = [0]
+    c_lc = to_lists(T.LC, T.SCC, T.HM, [0])
+    need("v", c_lc, s_h)
 
-    def send(ranks, dst, src_, sem):
-        cores = [T.cores[r] for r in ranks]
-        es = [e for e in topo.engines(core, cores[0]) if all(e in topo.engines(core, c) for c in cores)][:NE]
-        ids = [DstId(rid=topo.addr(c)[0], pnc=topo.addr(c)[1]) for c in cores]
-        g.remote_dma_fused([RemoteDMATransfer(dst_ids=ids, dma_engine_mask=sum(1 << e for e in es), remote_sem=T.sem[sem],
-                                              srcs=[src_], dsts=[dst for _ in cores])], local_sem=T.sem.ls)
-        sent[0] += len(es)
-    if peers:
-        need("q", c_m)
-        send([mine[i] for i in peers], T.MW[:, 128 * j:128 * j + 128], T.MW[:, 128 * j:128 * j + 128], "e1_%d" % j)
+    def slot_l(r):
+        return T.LL[:, 8 * r:8 * r + 8]
+    if rank + 1 < NR:
+        c_m = vcopy(T.MM[:], T.HM[:, 128:256].indirect(T.LC[:]))
+        need("v", c_m)
+        c_lm = to_lists(slot_l(rank), T.SCM, T.MM, [0])
+        need("q", c_lm)
+        send("e1", later(rank), slot_l(rank), lambda d: slot_l(rank))
 
     def region(s):
         return T.PW[:, 128 * s:128 * s + 128]
@@ -237,88 +274,73 @@ def rank_program(g, core, T, topo):
     ts(region(4), T.W0[:, 0:128], ms[4], OP.mult)
     ts(region(2), T.QM[:, 0:128], ms[2], OP.mult)
     ts(region(1), T.HM[:, 0:128], ms[1], OP.mult)
-    need("v", c_lc)
-    ts(region(5), T.W0[:, 128:256].indirect(T.LC[:]), -128.0, OP.add, ms[5], OP.mult)
+    ts(region(5), T.W0[:, 128:256].indirect(T.LC[:]), ms[5], OP.mult)
     need("v", s_m6)
-    c_p = ts(region(7), T.M6[:].indirect(T.LC[:]), -128.0, OP.add, ms[7], OP.mult)
+    c_p = ts(region(7), T.M6[:].indirect(T.LC[:]), ms[7], OP.mult)
     need("v", dem)
     a = ts(T.EI0[:], T.EM[:], 63, OP.bitwise_and)
     b = ts(T.EI1[:], T.EM[:], 6, OP.arith_shift_right)
-    ts(T.DB[:, :, 0, :], T.X[:], 128.0, OP.is_lt, -128.0, OP.mult)
-    ts(T.DB[:, :, 1, :], T.X[:], 256.0, OP.is_lt, -128.0, OP.mult)
-    need("v", a)
-    vcopy(T.EB[:, :, 0, :], T.EI0[:])
-    need("v", b)
-    c_eb = vcopy(T.EB[:, :, 1, :], T.EI1[:])
+    x0 = ts(T.DB[:, 0], T.X[:], 128.0, OP.is_lt, -128.0, OP.mult)
+    x1 = ts(T.DB[:, 1], T.X[:], 256.0, OP.is_lt, -128.0, OP.mult)
+    need("v", a, x0)
+    tt(T.EB[:, :, 0, :], T.EI0[:], T.DB[:, 0], OP.add)
+    need("v", b, x1)
+    c_eb = tt(T.EB[:, :, 1, :], T.EI1[:], T.DB[:, 1], OP.add)
     need("t", c_eb)
     for k in range(4):
         bank = T.PE0 if k < 2 else T.PE1
         for t in range(2):
-            o = bank[64 * t:64 * t + 64, 256 * (k % 2):256 * (k % 2) + 256]
-            mm(o, T.LS[:, t, k, :], T.EB[:, t], True, False)
-            p_e = mm(o, T.LS[:, t, k, :], T.DB[:, t], False, True)
+            p_e = mm(bank[64 * t:64 * t + 64, 256 * (k % 2):256 * (k % 2) + 256], T.LS[:, t, k, :], T.EB[:, t])
         if k % 2:
             need("s", p_e)
             s_ew = did("s", S.activation(T.EW[:, 256 * (k - 1):256 * (k - 1) + 512], bank[:], ACT.Relu, bias=1.0))
     own = SL * (1 + j)
     need("v", c_lt8)
-    c_mk = ts(T.MK[:], T.J16[:, 0:128], q_, OP.is_equal, T.LT8[:], OP.mult)
-    c_rst = ts(T.RST[:], T.J16[:, 0:128], 0.0, OP.not_equal)
+    c_mk = ts(T.MK[:], T.J16[:], q_, OP.is_equal, T.LT8[:], OP.mult)
+    c_rst = ts(T.RST[:], T.J16[:], 0.0, OP.not_equal)
     c_io1 = ts(T.IO1[:], T.IR[:, 0:64], 1.0, OP.add)
-    ts(T.MGP[:], T.IR[:, 0:8], gp_, OP.is_equal)
-    need("v", k_tr)
-    a = tt(T.TM[:], T.MS[:], T.TR[:], OP.mult)
     fill(T.F[:, own:own + 48], -1.0)
     fill(T.F[:, own + 112:own + 128], -1.0)
+    if first or j == 0:
+        fill(T.F[:, own - 16:own], 0.0)
+    fill(T.NB[:, 8 * rank:8 * rank + 8], 0.0)
     c_f = fill(T.F[:, own + 128:own + SL], 0.0)
-    need("v", a)
-    a = did("v", V.tensor_reduce(T.TP[:], T.TM[:], AX.X, OP.add))
     lists = [(1 + j, "own")]
     if rank > 0:
         lists.append((j, "prev"))
-    if rank + 1 < len(T.cores):
+    if rank + 1 < NR:
         lists.append((2 + j, "next"))
     w0 = min(x for x, _ in lists)
     w1 = max(x for x, _ in lists)
     for i, (x, _) in enumerate(lists):
         c_qi = ts(T.QI[:, 2 * i:2 * i + 2], T.IR[:, 0:17:16], q_, OP.add, float(SL * (x - w0) + 48 + 32 * rank), OP.add)
-    need("v", a)
-    c_tl = ts(T.TL[:], T.TR[:], T.TP[:], OP.is_gt)
-    need("s", c_tl)
-    for gg in range(8):
-        s_tri = scopy(T.TRI[:, 16 * gg:16 * gg + 16], T.TL[:], scale=T.MGP[:, gg:gg + 1])
 
-    def look(i, off):
-        if i != j:
-            need("v", ("e1_%d" % i, NE))
-        return T.MW[:, 128 * i:128 * i + 128].indirect(off)
-    if first:
-        c = None
-        for i in range(len(mine)):
-            if i == 0:
-                need("v", c_m if j == 0 else ("e1_0", NE))
-                c = vcopy(T.CUR[:, 0:1], T.MW[:, 0:1])
-            else:
-                need("v", c, c_m)
-                c = vcopy(T.CUR[:, 16 * i:16 * i + 16], look(i, T.CUR[:, 16 * (i - 1):16 * (i - 1) + 1]))
-        need("q", c)
-        send([rest[j]], T.X4[:], T.CUR[:, 48:50], "x4")
-        if j == 0:
-            c_po = vcopy(T.POFF[:, 0:1], T.QO[:])
+    if rank == 0:
+        c_po = vcopy(T.POFF[:, 0:1], T.QO[:])
+
+    def fold(e, lst):
+        win, c = T.IR[:], k_ir
+        for i in lst:
+            need(e, arrive("e1", i))
+            o = T.FB[:, 128 * i:128 * i + 128]
+            c = (vcopy if e == "v" else scopy)(o, win.indirect(slot_l(i)))
+            need(e, c)
+            win = o
+        return win, c
+    need("s", k_ir)
+    if rank > 0:
+        zero = T.LL[:, 0:1]
+        if first or j == 0:
+            win, c = fold("v", list(range(rank - 1, 0, -1)))
+            need("v", arrive("e1", 0))
         else:
-            c_po = ts(T.POFF[:, 0:1], T.CUR[:, 16 * (j - 1):16 * (j - 1) + 1], T.QO[:], OP.add)
-    else:
-        need("v", ("x4", NE))
-        off = T.X4[:, 0:1]
-        if j == 0:
-            c_po = ts(T.POFF[:, 0:1], off, T.QO[:], OP.add)
-        for i in range(j):
-            if i + 1 < j:
-                c = vcopy(T.CUR[:, 16 * i:16 * i + 16], look(i, off))
-                need("v", c)
-                off = T.CUR[:, 16 * i:16 * i + 1]
-            else:
-                c_po = ts(T.POFF[:], look(i, off), T.QO[:], OP.add)
+            far, c = fold("s", list(range(mine[0] - 1, 0, -1)))
+            win, _ = fold("v", list(range(rank - 1, mine[0] - 1, -1)))
+            need("v", arrive("e1", 0), c)
+            a = vcopy(T.X4[:], far.indirect(zero))
+            need("v", a)
+            zero = T.X4[:, 0:1]
+        c_po = ts(T.POFF[:], win.indirect(zero), T.QO[:], OP.add)
     need("s", c_po, c_p, s_p)
     st = scopy(T.JK[:], T.PW[:].indirect(T.POFF[:, 0:1]), accum_out=T.ST[:, 0:1])
     need("v", p_tt)
@@ -346,8 +368,7 @@ def rank_program(g, core, T, topo):
     need("v", p_n, c_inc)
     a = ts(T.POS[:], T.INC[:], T.PSO[:, 0:1], OP.add)
     need("v", c_f)
-    vcopy(T.NOW[:], T.PSO[:, 1:2])
-    c_n = vcopy(T.F[:, own + 128:own + 129], T.PSO[:, 1:2])
+    c_n = vcopy(T.NB[:, 8 * rank:8 * rank + 1] if first else T.F[:, own + 128:own + 129], T.PSO[:, 1:2])
     need("v", a, c_io1)
     for i in range(8):
         a = ts(T.OH[:, i, :], T.IO1[:], T.POS[:, i:i + 1], OP.is_equal, T.SCN[:, 16 * i + 15:16 * i + 16], OP.mult)
@@ -355,60 +376,50 @@ def rank_program(g, core, T, topo):
         p_a = mm(T.PSA[:, 256:320], T.BO[:], T.OH[:, i, :], i == 0, i == 7)
     need("v", p_a)
     c_a = ts(T.F[:, own + 48:own + 112], T.PSA[:, 256:320], -1.0, OP.add)
+    c_now = vcopy(T.NOW[:], T.PSO[:, 1:2])
 
     def part(x, lo, hi):
         return T.F[:, SL * x + lo:SL * x + hi]
+    wide = 128 if first else SL
+
+    def slot_f(d):
+        return part(1 + j if d in mine else (0 if d > rank else 1 + len(mine)), 0, wide)
     if first:
         need("q", c_n)
-        send([r for r in mine if r != rank], part(1 + j, 128, SL), part(1 + j, 128, SL), "en_%d" % j)
-        need("q", c_a)
-        if j + 1 == len(mine):
-            send([rank + 1], part(0, 0, SL), part(1 + j, 0, SL), "eo")
-        near = [r for r in mine if abs(r - rank) == 1]
-        send(near, part(1 + j, 0, 128), part(1 + j, 0, 128), "ev_%d" % j)
-        for i in range(len(mine)):
-            if i != j:
-                need("v", ("en_%d" % i, NE))
-        need("v", c_n)
-        x0 = SL + 128
-        c_4 = did("v", V.tensor_reduce(T.C4S[:], T.F[:, x0:x0 + 3 * SL + 1:SL], AX.X, OP.add))
-        need("q", c_4)
-        send([rest[j]], T.C4[:], T.C4S[:], "c4")
-    else:
-        need("q", c_a, c_n)
-        near = [r for r in mine if r > rank or r == rank - 1]
-        send(near, part(1 + j, 0, SL), part(1 + j, 0, SL), "ev_%d" % j)
-        if j == 0:
-            send([rank - 1], part(1 + len(mine), 0, 128), part(1, 0, 128), "eo")
+        send("en", later(rank), T.NB[:, 8 * rank:8 * rank + 8], lambda d: T.NB[:, 8 * rank:8 * rank + 8])
+    need("q", c_a, c_n)
+    send("ev", e2(rank), part(1 + j, 0, wide), slot_f)
 
-    if first:
-        got = [i for i in range(len(mine)) if abs(i - j) == 1]
-    else:
-        got = [i for i in range(len(mine)) if i < j or i == j + 1]
-    for i in got:
-        need("v", ("ev_%d" % i, NE))
-    if (first and j + 1 == len(mine)) or (not first and j == 0):
-        need("v", ("eo", NE))
-    x0 = SL + 128
+    for i in range(rank):
+        if same(i, 0):
+            need("v", arrive("en", i))
+    if not first:
+        c_4 = did("v", V.tensor_reduce(T.C4[:], T.NB[:, 0:8 * mine[0] - 7:8], AX.X, OP.add))
+    for i in range(rank):
+        if rank in e2(i):
+            need("v", arrive("ev", i))
     beg = 0.0
     if rank > 0:
-        c_np = vcopy(T.NPV[:], part(j, 128, 129))
+        c_np = vcopy(T.NPV[:], T.NB[:, 8 * rank - 8:8 * rank - 7] if first or j == 0 else part(j, 128, 129))
+    if j > 1:
+        a = did("v", V.tensor_reduce(T.BG0[:], T.NB[:, 0:8 * j - 7:8] if first
+                                     else T.F[:, SL + 128:SL + 129 + SL * (j - 1):SL], AX.X, OP.add))
+    if rank > 0:
         need("v", c_np)
     if j == 1:
         beg = T.NPV[:]
     elif j > 1:
-        a = did("v", V.tensor_reduce(T.BG0[:], T.F[:, x0:x0 + SL * (j - 1) + 1:SL], AX.X, OP.add))
         need("v", a)
         beg = T.BG0[:]
     if not first:
-        need("v", ("c4", NE))
+        need("v", c_4)
         if j == 0:
             beg = T.C4[:]
         else:
             a = tt(T.BG[:], T.C4[:], beg, OP.add)
             need("v", a)
             beg = T.BG[:]
-    need("v", c_qi, c_a, c_n)
+    need("v", c_qi, c_a, c_n, c_now)
     for i, (x, what) in enumerate(lists):
         o, q2 = T.OF2[:, 2 * i:2 * i + 2], T.QI[:, 2 * i:2 * i + 2]
         if what == "own":
@@ -419,6 +430,8 @@ def rank_program(g, core, T, topo):
             a = ts(o, q2, beg, OP.subtract, T.NOW[:], OP.subtract)
     n = len(lists)
     need("v", a)
+    if rank + 1 < NR:
+        need("v", arrive("ev", rank + 1))
     a = vcopy(T.YG[:, 0:32 * n], T.F[:, SL * w0:SL * w1 + 128].indirect(T.OF2[:, 0:2 * n]))
     need("v", a)
     out = T.Y1

@@ -1,16 +1,17 @@
 from concourse.bass import DstId, RemoteDMATransfer
 from concourse.mybir import dt, AluOpType, AxisListType, ActivationFunctionType
 
-SL = 144
 _BUF = {
-    "int32": "PI:1 CI:8 SYI:2x2x2x4 X:2x128 XA:2x128 EM:2x128 EI0:2x128 EI1:2x128",
-    "uint16": "LST:192 LA:32 LB:16 LC:8 LL:64 POFF:16 X4:16 OFP:8 OF2:6",
-    "float32": "CF:8 RI:256 IR:128 GC:128 J16:128 BR:192 TR:16 MG:4 MS:16 MGP:8 QO:1 LT8:1 Q1:1 CORR:1 SD0:128 SD1:128 "
-               "TM:16 TP:1 QI:6 LSF:192 JK:16 ST:4 TA:3x128 C4:1 BG0:1 BG:1 NPV:1 NOW:1 YG:96 Y1:32 Y2:32",
-    "bfloat16": "R:256 XR:128 BO:128 RB:8x128 ONE:128 IO1:64 TL:16 TRI:128 SYB:2x2x2x4 XT:2x128 XS:2x128 EB:2x2x128 "
-                "DB:2x2x128 SEL:2x4x8 LS:2x4x64 YB:16x64 T3:128 W3:1024 W2:1024 W1:1024 W0:1024 QM:512 HM:256 MM:128 "
-                "SD:128 SCA:512 SCB:256 SCC:128 SCM:128 FB:896 M6:128 PW:1152 EW:1024 MK:128 RST:128 GV:128 SCN:128 "
-                "FL:8 INC:8 POS:8 OH:8x64 NB:64 F:%d" % (6 * SL),
+    "int32": "PI:1 CI:4 SYI:2x32 X:2x128 XA:2x128 EM:2x128 EI0:2x128",
+    "uint16": "LST:3x64 LA:32 LB:16 LC:8 LL:64 X1:16 X4:16 OFP:4 OF2:2",
+    "float32": "PF:1 CF:4 RI:128 IR:128 GC:128 J16:128 KEY:128 MG:4 MS:16 S0:16 Q1:1 CORR:1 MU:1 M1:1 K1:1 KP:1 RA:1 S1:1 "
+               "SD0:128 SD1:128 KC:4 EMF:2x128 EA:2x128 QI:2 ST:2 TA:2x128 NV:4 OWN:1 BEG:1 A1:1 B1:1 U:2 U1:2 U2:2 U3:2 "
+               "U4:2 Y1:32",
+    "bfloat16": "R:128 XR:128 BRR:192 DG:8x128 ZB:128 G4:128 R3:128 BO:128 RB:8x128 ONE:128 IO1:64 TU:128 TRI:128 "
+                "SYB:2x32 XT:2x128 XS:2x128 XB:2x128 EB:2x2x128 SG:2x2x128 SEL:4x2x8 LS:4x2x64 LSH:2x2x64 YB:16x64 T3:128 "
+                "T1:128 WH:1024 HH:1024 W3:1024 W2:1024 W1:1024 W0:1024 QM:512 HM:256 MM:128 SD:128 SCA:512 SCB:256 "
+                "SCC:128 SCM:128 FB:896 M6:128 PW:128 EW:512 MK:64 RST:64 GV:64 SCN:64 FL:64 INC:64 POS:4 OH:4x64 OD:64 "
+                "NB:64 F:192",
 }
 SCRATCH = {n: ("sbuf", [128] + [int(x) for x in d.split("x")], t)
            for t, l in _BUF.items() for n, d in (w.split(":") for w in l.split())}
@@ -60,16 +61,20 @@ def rank_program(g, core, T, topo):
     def fill(ap, x):
         return did("v", V.memset(ap, x))
 
+    def scan(out, d0, d1, o0, o1):
+        return did("v", V.tensor_tensor_scan(out, d0, d1, 0.0, o0, o1))
+
+    def act(out, in_, func, **k):
+        return did("s", S.activation(out, in_, func, **k))
+
     def scopy(out, in_, **k):
-        return did("s", S.activation(out, in_, ACT.Copy, **k))
+        return act(out, in_, ACT.Copy, **k)
 
     def mm(out, lhsT, rhs, start=True, stop=True):
         return did("t", PE.matmul(out, lhsT, rhs, start, stop))
 
-    def iota(out, pattern, cm=0):
-        if cm:
-            return did("q", g.iota(out, pattern, 0, cm))
-        return did("q", g.iota(out, pattern, 0, cm, allow_small_or_imprecise_dtypes=True))
+    def iota(out, pattern, cm=0, base=0):
+        return did("q", g.iota(out, pattern, base, cm, allow_small_or_imprecise_dtypes=True))
 
     def same(r, r2):
         return topo.chip(T.cores[r]) == topo.chip(T.cores[r2])
@@ -90,12 +95,11 @@ def rank_program(g, core, T, topo):
     def later(r):
         return list(range(NR - 1, r, -1))
 
-    def e2(r):
-        d = [x for x in range(NR) if abs(x - r) == 1]
-        return d if same(r, 0) else d + [x for x in later(r) if x not in d]
+    def beside(r):
+        return [x for x in range(NR) if abs(x - r) == 1]
 
     def arrive(kind, r):
-        dsts = e2(r) if kind == "ev" else later(r)
+        dsts = beside(r) if kind == "ev" else later(r)
         return ("%s_%d" % (kind, r), [len(es) for ds, es in plan(r, dsts) if rank in ds][0])
     sent = [0]
 
@@ -109,146 +113,159 @@ def rank_program(g, core, T, topo):
             sent[0] += len(es)
         g.remote_dma_fused(trs, local_sem=T.sem.ls)
 
-    g.sync.dma_start(T.SYI[0:8], T.sy[:, :]).then_inc(T.sem.dsy, 16)
     g.sync.dma_start(T.X[:, 0, :], T.nx[0:4, :]).then_inc(T.sem.dx, 16)
     S.dma_start(T.X[:, 1, :], T.nx[4:8, :]).then_inc(T.sem.dxs, 16)
+    g.sync.dma_start(T.SYI[0:4, 0, :], T.sy[0:4, :]).then_inc(T.sem.dsy, 16)
+    S.dma_start(T.SYI[0:4, 1, :], T.sy[4:8, :]).then_inc(T.sem.dsy, 16)
     g.sync.dma_start(T.EM[:, 0, :], T.em[0:4, :]).then_inc(T.sem.dem, 16)
     g.sync.dma_start(T.EM[:, 1, :], T.em[4:8, :]).then_inc(T.sem.dem, 16)
-    dsy, dx, dxs, dem = ("dsy", 16), ("dx", 16), ("dxs", 16), ("dem", 32)
+    dsy, dx, dxs, dem = ("dsy", 32), ("dx", 16), ("dxs", 16), ("dem", 32)
 
-    k_pi = iota(T.PI[:], [[0, 1]], 1)
-    k_ri = iota(T.RI[0:8, :], [[1, 8], [0, 32]])
-    k_ir = iota(T.IR[:], [[1, 128]])
+    k_pi = did("q", g.iota(T.PI[:], [[0, 1]], 0, 1))
     k_gc = iota(T.GC[:], [[1, 8], [0, 16]])
-    iota(T.TR[:, 0:8], [[1, 2], [2, 2], [4, 2]])
-    k_tr = iota(T.TR[:, 8:16], [[1, 2], [2, 2], [4, 2]])
+    k_ir = iota(T.IR[:], [[1, 128]])
+    k_ri = iota(T.RI[0:4, :], [[1, 4], [0, 32]])
+    k_pf = iota(T.PF[:], [[0, 1]], 1)
     k_j16 = iota(T.J16[:], [[0, 8], [1, 16]])
-    k_br = iota(T.BR[:], [[0, 6], [128, 4], [0, 8]])
-    k_xr = iota(T.XR[0:1, :], [[1, 128]])
+    k_br = iota(T.BRR[0:1, :], [[0, 6], [128, 4], [0, 8]])
+    k_xr = iota(T.XR[:], [[1, 128]])
+    k_key = iota(T.KEY[:], [[0, 8], [1, 2], [2, 8]])
+    k_kc = iota(T.KC[:], [[128, 4]])
 
     c_ls0 = fill(T.LS[:], 0.0)
-    c_one = fill(T.ONE[:], 1.0)
     need("v", k_pi)
-    ts(T.CI[:, 0:1], T.PI[:], 15, OP.bitwise_and)
-    ts(T.CI[:, 1:2], T.PI[:], 31, OP.bitwise_and)
-    ts(T.CI[:, 2:3], T.PI[:], 5, OP.arith_shift_right)
-    ts(T.CI[:, 3:4], T.PI[:], 4, OP.arith_shift_right)
-    a = vcopy(T.CI[:, 4:5], T.PI[:])
+    for i, (x, op) in enumerate(((15, OP.bitwise_and), (31, OP.bitwise_and), (5, OP.arith_shift_right),
+                                 (4, OP.arith_shift_right))):
+        a = ts(T.CI[:, i:i + 1], T.PI[:], x, op)
     need("v", a)
-    c_cf = vcopy(T.CF[:, 0:5], T.CI[:, 0:5])
-    q_, a_, gt_, gp_, p_ = [T.CF[:, i:i + 1] for i in range(5)]
-    need("v", c_cf, k_ri)
-    c_r = ts(T.R[0:8, :], T.RI[0:8, :], T.CF[0:8, 4:5], OP.is_equal)
-    need("v", k_ir)
-    c_mg = ts(T.MG[:], T.IR[:, 0:4], gt_, OP.is_equal)
-    c_ms = ts(T.MS[:], T.IR[:, 0:16], q_, OP.is_equal)
-    need("v", k_gc)
+    c_cf = vcopy(T.CF[:], T.CI[:])
+    q_, a_, gt_, gp_ = [T.CF[:, i:i + 1] for i in range(4)]
+    need("v", c_cf, k_gc)
     c_bo = ts(T.BO[:], T.GC[:], gp_, OP.is_equal)
-    ts(T.QO[:], q_, 128.0, OP.mult, 1024.0, OP.min)
-    ts(T.CORR[:], q_, 15.0, OP.is_lt, -128.0, OP.mult)
-    ts(T.Q1[:], q_, 1.0, OP.add)
-    ts(T.MGP[:], T.IR[:, 0:8], gp_, OP.is_equal)
-    c_lt8 = ts(T.LT8[:], q_, 8.0, OP.is_lt)
+    c_mu = ts(T.MU[:], q_, 8.0, OP.is_ge)
+    ts(T.M1[:], q_, 8.0, OP.is_lt)
+    need("v", k_ir)
+    c_ms = ts(T.MS[:], T.IR[:, 0:16], q_, OP.is_equal)
+    c_mg = ts(T.MG[:], T.IR[:, 0:4], gt_, OP.is_equal)
+    c_one = fill(T.ONE[:], 1.0)
+    need("v", c_mu)
+    c_k1 = ts(T.K1[:], T.MU[:], -15.0, OP.mult)
     need("s", c_bo, c_ms)
     for b in range(8):
-        c_rb = scopy(T.RB[:, b, :], T.BO[:], scale=T.MS[:, b:b + 1])
-
+        s_rb = scopy(T.RB[:, b, :], T.BO[:], scale=T.MS[:, b:b + 1])
+    need("v", c_k1)
+    c_kp = ts(T.KP[:], q_, 2.0, OP.mult, T.K1[:], OP.add)
+    need("v", k_ri, k_pf)
+    c_r = ts(T.R[0:4, :], T.RI[0:4, :], T.PF[0:4, :], OP.is_equal)
     need("v", dsy)
-    for e in range(2):
-        for h in range(2):
-            c_syb = vcopy(T.SYB[0:8, e, :, h, :], T.SYI[0:8, h, :, e, :])
+    c_syb = vcopy(T.SYB[0:4], T.SYI[0:4])
     need("t", c_syb, c_r)
-    for t in range(2):
-        p_rep = mm(T.PSA[:, 32 * t:32 * t + 32], T.R[0:8, 128 * t:128 * t + 128], T.SYB[0:8])
+    for k in range(4):
+        p_rep = mm(T.PSA[:, 16 * k:16 * k + 16], T.R[0:4, :], T.SYB[0:4, :, k:32:4])
     need("v", dx, dxs)
     a = ts(T.XA[:], T.X[:], 127, OP.bitwise_and)
     need("v", p_rep)
-    for k in range(4):
-        c_sel = ts(T.SEL[:, :, k, :], T.PSA[:, k:64:4], a_, OP.is_equal)
+    c_sel = ts(T.SEL[:], T.PSA[:, 0:64], a_, OP.is_equal)
     need("v", a)
     c_xt = vcopy(T.XT[:], T.XA[:])
-    need("v", c_sel, c_mg, c_ls0)
+    need("s", c_sel, c_mg, c_ls0)
     for gg in range(4):
-        c_ls = ts(T.LS[:, :, :, 16 * gg:16 * gg + 8], T.SEL[:], T.MG[:, gg:gg + 1], OP.mult)
-    need("t", c_ls, c_xt)
+        s_ls = scopy(T.LS[:, :, :, 16 * gg:16 * gg + 8], T.SEL[:], scale=T.MG[:, gg:gg + 1])
+    need("t", s_ls, c_xt)
     for t in range(2):
-        p_t3 = mm(T.PSA[64 * t:64 * t + 64, 128:256], T.LS[:, t, 3, :], T.XT[:, t, :])
-    need("s", c_xt, c_mg)
-    for gg in range(2):
-        s_yb = scopy(T.YB[:, :, 16 * gg:16 * gg + 16], T.XT[:], scale=T.MG[:, gg:gg + 1])
-    need("v", c_xt)
-    for gg in range(2, 4):
-        c_yb = ts(T.YB[:, :, 16 * gg:16 * gg + 16], T.XT[:], T.MG[:, gg:gg + 1], OP.mult)
-    need("v", p_t3)
-    c_t3 = vcopy(T.T3[:], T.PSA[:, 128:256])
-    s_xs = scopy(T.XS[:], T.XT[:], scale=1.0 / 512.0)
-    need("t", c_t3, c_rb)
-    for b in range(4):
-        p_wa = mm(T.PWA[:, 128 * b:128 * b + 128], T.RB[:, b, :], T.T3[:])
-    need("t", c_yb, s_yb, c_sel)
+        p_t3 = mm(T.PSA[64 * t:64 * t + 64, 128:256], T.LS[:, 3, t, :], T.XT[:, t, :])
+    need("s", p_t3)
+    s_t3 = scopy(T.T3[:], T.PSA[:, 128:256])
+    need("v", c_xt, c_mg)
+    c_yb = []
     for t in range(2):
+        for gg in range(4):
+            a = ts(T.YB[:, 8 * t:8 * t + 8, 16 * gg:16 * gg + 16], T.XT[:, t, :], T.MG[:, gg:gg + 1], OP.mult)
+        c_yb.append(a)
+
+    def lists(t):
+        need("t", c_one, k_br)
+        mm(T.PSL[64 * t:64 * t + 64, 0:24, :], T.ONE[0:1, 0:64], T.BRR[0:1, :], True, False)
+        need("t", c_yb[t], c_sel)
         for c in range(8):
-            p_l = mm(T.PSL[64 * t:64 * t + 64, 0:24, c], T.YB[:, 8 * t + c, :], T.SEL[:, t, 0:3, :])
+            x = mm(T.PSL[64 * t:64 * t + 64, 0:24, c], T.YB[:, 8 * t + c, :], T.SEL[:, 0:3, t, :], False, c == 7)
+        return x
+    lists(0)
+    need("t", s_t3, s_rb)
     for b in range(4):
         p_wb = mm(T.PWB[:, 128 * b:128 * b + 128], T.RB[:, 4 + b, :], T.T3[:])
-    need("t", s_xs, k_xr, c_one)
+    for b in range(3):
+        p_wa = mm(T.PWA[:, 128 * b:128 * b + 128], T.RB[:, b, :], T.T3[:])
+    p_w3 = mm(T.PSO[:, 0:128], T.RB[:, 3, :], T.T3[:])
+    p_l = lists(1)
     for t in range(2):
-        for k in range(3):
-            mm(T.PTT[64 * t:64 * t + 64, k, :], T.ONE[0:1, 0:64], T.XR[0:1, :], True, False)
-            p_tt = mm(T.PTT[64 * t:64 * t + 64, k, :], T.LS[:, t, k, :], T.XS[:, t, :], False, True)
-    need("v", k_tr)
-    a = tt(T.TM[:], T.MS[:], T.TR[:], OP.mult)
-    need("v", k_j16)
-    x0 = ts(T.SD0[:], T.J16[:], q_, OP.is_equal, -65536.0, OP.mult)
-    need("v", a)
-    a = did("v", V.tensor_reduce(T.TP[:], T.TM[:], AX.X, OP.add))
-    x1 = ts(T.SD1[:], T.J16[:], T.Q1[:], OP.is_equal, 128.0, OP.mult)
-    need("v", a)
-    c_tl = ts(T.TL[:], T.TR[:], T.TP[:], OP.is_gt)
-    need("s", c_tl)
-    for gg in range(8):
-        s_tri = scopy(T.TRI[:, 16 * gg:16 * gg + 16], T.TL[:], scale=T.MGP[:, gg:gg + 1])
-    need("v", p_wa)
-    c_w = vcopy(T.W3[:, 0:512], T.PWA[:])
+        p_t1 = mm(T.PSA[64 * t:64 * t + 64, 320:448], T.LS[:, 1, t, :], T.XT[:, t, :])
     need("s", p_wb)
     s_w = scopy(T.W3[:, 512:1024], T.PWB[:])
+    need("s", p_w3)
+    s_w3 = scopy(T.W3[:, 384:512], T.PSO[:, 0:128])
+    need("s", p_t1)
+    s_t1 = scopy(T.T1[:], T.PSA[:, 320:448])
+    need("v", k_j16)
+    a = ts(T.Q1[:], q_, 1.0, OP.add)
+    x0 = ts(T.SD0[:], T.J16[:], q_, OP.is_equal, -65536.0, OP.mult)
+    need("v", a)
+    x1 = ts(T.SD1[:], T.J16[:], T.Q1[:], OP.is_equal, 128.0, OP.mult)
+    ts(T.CORR[:], q_, 15.0, OP.is_lt, -128.0, OP.mult)
     need("v", x0, x1)
     c_sd = tt(T.SD[:], T.SD0[:], T.SD1[:], OP.add)
-    need("v", p_l, k_br)
-    a = tt(T.LSF[:], T.PSL[:, 0:24, :], T.BR[:], OP.add)
-    need("v", a)
-    c_l = vcopy(T.LST[:], T.LSF[:])
+    need("v", p_wa)
+    c_w = vcopy(T.W3[:, 0:384], T.PWA[:, 0:384])
+    need("v", p_l)
+    c_l = vcopy(T.LST[:], T.PSL[:, 0:24, :])
+    need("t", s_t1, s_w, c_w)
+    for b in range(8):
+        p_wh = mm((T.PE1 if b > 3 else T.PWA)[:, 128 * (b % 4):128 * (b % 4) + 128], T.RB[:, b, :], T.T1[:])
+
+    need("q", c_bo, c_one, s_rb)
+    for b in (5, 6, 7, 4, 0, 1, 2, 3):
+        k_dg = did("q", g.affine_select(T.DG[:, b, :], T.RB[:, b, :], [[0, 8], [0, 2], [1, 8]], OP.is_equal, 0.0, -b, 0))
+    k_rst = did("q", g.affine_select(T.RST[:], T.ONE[:, 0:64], [[0, 4], [1, 16]], OP.not_equal, 0.0, 0, 0))
+    k_io1 = iota(T.IO1[:], [[1, 64]], 0, 1)
+    k_nb = iota(T.NB[:, 8 * rank:8 * rank + 8], [[0, 8]])
 
     src = T.W3
+    need("v", s_w3)
     for k, dst in ((2, T.W2), (1, T.W1), (0, T.W0)):
         need("v", c_w, c_l)
-        c_w = vcopy(dst[:, 0:512], src[:, 0:512].indirect(T.LST[:, 64 * k:64 * k + 32]))
         need("s", s_w, c_l)
-        s_w = scopy(dst[:, 512:1024], src[:, 512:1024].indirect(T.LST[:, 64 * k + 32:64 * k + 64]))
+        c_w = vcopy(dst[:, 0:512], src[:, 0:512].indirect(T.LST[:, k, 0:32]))
+        s_w = scopy(dst[:, 512:1024], src[:, 512:1024].indirect(T.LST[:, k, 32:64]))
         src = dst
 
-    def to_lists(lst, sc, win, slots):
-        for s in slots:
-            x = did("v", V.tensor_tensor_scan(sc[:, 128 * s:128 * s + 128], T.SD[:], win[:, 128 * s:128 * s + 128], 0.0,
-                                              OP.add, OP.max))
+    def to_lists(lst, sc, win, slots, at=0):
+        for i, s in enumerate(slots):
+            x = scan(sc[:, 128 * (at + i):128 * (at + i) + 128], T.SD[:], win[:, 128 * s:128 * s + 128], OP.add, OP.max)
         need("v", x)
-        s, n = slots[0], len(slots)
-        return ts(lst[:, 8 * s:8 * s + 8 * n], sc[:, 128 * s + 15:128 * (s + n):16], T.CORR[:], OP.add)
-    need("v", c_w, c_sd)
-    l1 = to_lists(T.LA, T.SCA, T.W0, [2, 3])
-    l0 = to_lists(T.LA, T.SCA, T.W0, [0, 1])
-    need("v", l0, s_w)
-    need("s", l1, s_w)
-    for s in range(2):
-        c_q = vcopy(T.QM[:, 128 * s:128 * s + 128], T.W0[:, 512 + 128 * s:640 + 128 * s].indirect(T.LA[:, 8 * s:8 * s + 8]))
-    for s in range(2, 4):
-        s_q = scopy(T.QM[:, 128 * s:128 * s + 128], T.W0[:, 512 + 128 * s:640 + 128 * s].indirect(T.LA[:, 8 * s:8 * s + 8]))
-    need("v", c_q)
-    c_lb = to_lists(T.LB, T.SCB, T.QM, [0, 1])
-    need("v", c_lb, s_q)
-    c_h = vcopy(T.HM[:, 0:128], T.QM[:, 256:384].indirect(T.LB[:, 0:8]))
-    need("s", c_lb, s_q)
-    s_h = scopy(T.HM[:, 128:256], T.QM[:, 384:512].indirect(T.LB[:, 8:16]))
+        n = len(slots)
+        return ts(lst[:, 8 * at:8 * at + 8 * n], sc[:, 128 * at + 15:128 * (at + n):16], T.CORR[:], OP.add)
+
+    def w0(b):
+        return T.W0[:, 128 * b:128 * b + 128]
+
+    def qm(b):
+        return T.QM[:, 128 * b:128 * b + 128]
+    need("v", c_w, s_w, c_sd)
+    l1 = to_lists(T.LA, T.SCA, T.W0, [4, 6], 2)
+    l0 = to_lists(T.LA, T.SCA, T.W0, [0, 2])
+    need("v", l0)
+    c_q = vcopy(qm(0), w0(1).indirect(T.LA[:, 0:8]))
+    need("s", l1)
+    s_q2 = scopy(qm(2), w0(5).indirect(T.LA[:, 16:24]))
+    s_q = scopy(qm(3), w0(7).indirect(T.LA[:, 24:32]))
+    need("s", l0)
+    s_q1 = scopy(qm(1), w0(3).indirect(T.LA[:, 8:16]))
+    need("v", c_q, s_q2)
+    c_lb = to_lists(T.LB, T.SCB, T.QM, [0, 2])
+    need("v", c_lb, s_q1)
+    c_h = vcopy(T.HM[:, 0:128], qm(1).indirect(T.LB[:, 0:8]))
+    need("s", c_lb, s_q1)
+    s_h = scopy(T.HM[:, 128:256], qm(3).indirect(T.LB[:, 8:16]))
     need("v", c_h)
     c_lc = to_lists(T.LC, T.SCC, T.HM, [0])
     need("v", c_lc, s_h)
@@ -262,64 +279,71 @@ def rank_program(g, core, T, topo):
         need("q", c_lm)
         send("e1", later(rank), slot_l(rank), lambda d: slot_l(rank))
 
-    def region(s):
-        return T.PW[:, 128 * s:128 * s + 128]
-    ms = [T.MS[:, s:s + 1] for s in range(8)]
-    s_m6 = scopy(T.M6[:], T.W0[:, 384:512].indirect(T.LB[:, 8:16]))
-    scopy(region(6), T.W0[:, 256:384].indirect(T.LB[:, 0:8]), scale=ms[6])
-    need("s", c_lc)
-    s_p = scopy(region(3), T.QM[:, 128:256].indirect(T.LC[:]), scale=ms[3])
-    ts(region(0), T.IR[:], ms[0], OP.mult)
-    fill(region(8), 0.0)
-    ts(region(4), T.W0[:, 0:128], ms[4], OP.mult)
-    ts(region(2), T.QM[:, 0:128], ms[2], OP.mult)
-    ts(region(1), T.HM[:, 0:128], ms[1], OP.mult)
-    ts(region(5), T.W0[:, 128:256].indirect(T.LC[:]), ms[5], OP.mult)
-    need("v", s_m6)
-    c_p = ts(region(7), T.M6[:].indirect(T.LC[:]), ms[7], OP.mult)
+    s_m6 = scopy(T.M6[:], w0(6).indirect(T.LB[:, 8:16]))
+    s_r3 = scopy(T.R3[:], w0(2).indirect(T.LB[:, 0:8]))
+
+    def choose(out, what):
+        for i, (b, win) in enumerate(what):
+            x = mm(out, T.DG[:, b, :], win, i == 0, i + 1 == len(what))
+        return x
+    need("t", s_m6, c_h, k_dg, k_xr, s_w, c_lc)
+    p_z = choose(T.PWB[:, 0:128], [(4, T.XR[:]), (5, w0(4)), (6, qm(2)), (7, T.M6[:])])
+    need("v", p_wh)
+    c_wh = vcopy(T.WH[:, 0:512], T.PWA[:])
+    need("s", p_wh)
+    s_wh = scopy(T.WH[:, 512:1024], T.PE1[:])
+    need("s", p_z)
+    s_z = scopy(T.ZB[:], T.PWB[:, 0:128])
+    need("s", c_xt, c_sel, c_mg)
+    s_xs = scopy(T.XS[:], T.XT[:], scale=1.0 / 512.0)
+    for gg in range(4):
+        for u in range(2):
+            s_lh = scopy(T.LSH[:, :, :, 16 * gg + 8 * u:16 * gg + 8 * u + 8], T.SEL[:, 2 * u:2 * u + 2], scale=T.MG[:, gg:gg + 1])
+    c_xb = vcopy(T.XB[:], T.X[:])
+    need("v", s_z)
+    c_g4 = vcopy(T.G4[:], T.ZB[:].indirect(T.LC[:]))
+    need("t", s_xs, k_xr, c_one, s_lh)
+    for t in range(2):
+        mm(T.PTT[64 * t:64 * t + 64, 1, :], T.ONE[0:1, 0:64], T.XR[0:1, :], True, False)
+        p_tt = mm(T.PTT[64 * t:64 * t + 64, 1, :], T.LSH[:, 0, t, :], T.XS[:, t, :], False, True)
+    need("t", c_g4, s_r3)
+    p_pw = choose(T.PWB[:, 128:256], [(0, T.XR[:]), (1, w0(0)), (2, qm(0)), (3, T.R3[:])]
+                  + [(b, T.G4[:]) for b in (4, 5, 6, 7)])
     need("v", dem)
+    c_em = ts(T.EMF[:], T.EM[:], -31.5, OP.add)
     a = ts(T.EI0[:], T.EM[:], 63, OP.bitwise_and)
-    b = ts(T.EI1[:], T.EM[:], 6, OP.arith_shift_right)
-    x0 = ts(T.DB[:, 0], T.X[:], 128.0, OP.is_lt, -128.0, OP.mult)
-    x1 = ts(T.DB[:, 1], T.X[:], 256.0, OP.is_lt, -128.0, OP.mult)
-    need("v", a, x0)
-    tt(T.EB[:, :, 0, :], T.EI0[:], T.DB[:, 0], OP.add)
-    need("v", b, x1)
-    c_eb = tt(T.EB[:, :, 1, :], T.EI1[:], T.DB[:, 1], OP.add)
-    need("t", c_eb)
-    for k in range(4):
-        bank = T.PE0 if k < 2 else T.PE1
+    need("s", c_xb)
+    act(T.SG[:, :, 0, :], T.XB[:], ACT.Sign, bias=-127.5)
+    act(T.SG[:, :, 1, :], T.XB[:], ACT.Sign, bias=-255.5)
+    need("v", a)
+    c_eb = ts(T.EB[:, :, 0, :], T.EI0[:], 1.0 / 64.0, OP.mult)
+    need("s", c_em)
+    a = scopy(T.EA[:], T.EMF[:], scale=1.0 / 64.0, bias=12582912.0)
+    need("s", a)
+    s_eb = scopy(T.EB[:, :, 1, :], T.EA[:], scale=1.0 / 64.0, bias=-196608.0)
+    need("t", c_eb, s_eb)
+    for k in range(2):
         for t in range(2):
-            p_e = mm(bank[64 * t:64 * t + 64, 256 * (k % 2):256 * (k % 2) + 256], T.LS[:, t, k, :], T.EB[:, t])
-        if k % 2:
-            need("s", p_e)
-            s_ew = did("s", S.activation(T.EW[:, 256 * (k - 1):256 * (k - 1) + 512], bank[:], ACT.Relu, bias=1.0))
-    own = SL * (1 + j)
-    need("v", c_lt8)
-    c_mk = ts(T.MK[:], T.J16[:], q_, OP.is_equal, T.LT8[:], OP.mult)
-    c_rst = ts(T.RST[:], T.J16[:], 0.0, OP.not_equal)
-    c_io1 = ts(T.IO1[:], T.IR[:, 0:64], 1.0, OP.add)
-    fill(T.F[:, own:own + 48], -1.0)
-    fill(T.F[:, own + 112:own + 128], -1.0)
-    if first or j == 0:
-        fill(T.F[:, own - 16:own], 0.0)
-    fill(T.NB[:, 8 * rank:8 * rank + 8], 0.0)
-    c_f = fill(T.F[:, own + 128:own + SL], 0.0)
-    lists = [(1 + j, "own")]
-    if rank > 0:
-        lists.append((j, "prev"))
-    if rank + 1 < NR:
-        lists.append((2 + j, "next"))
-    w0 = min(x for x, _ in lists)
-    w1 = max(x for x, _ in lists)
-    for i, (x, _) in enumerate(lists):
-        c_qi = ts(T.QI[:, 2 * i:2 * i + 2], T.IR[:, 0:17:16], q_, OP.add, float(SL * (x - w0) + 48 + 32 * rank), OP.add)
+            o = T.PE0[64 * t:64 * t + 64, 256 * k:256 * k + 256]
+            mm(o, T.LSH[:, k, t, :], T.SG[:, t], True, False)
+            p_e = mm(o, T.LSH[:, k, t, :], T.EB[:, t], False, True)
+    need("v", c_wh)
+    c_hh = ts(T.HH[:, 0:512], T.WH[:, 0:512].indirect(T.LST[:, 0, 0:32]), 1.0 / 512.0, OP.mult)
+    need("s", s_wh)
+    s_hh = scopy(T.HH[:, 512:1024], T.WH[:, 512:1024].indirect(T.LST[:, 0, 32:64]), scale=1.0 / 512.0)
+    need("t", c_hh, s_hh)
+    mm(T.PTT[:, 0, :], T.ONE[0:1, :], T.XR[0:1, :], True, False)
+    for b in range(8):
+        p_ta = mm(T.PTT[:, 0, :], T.DG[:, b, :], T.HH[:, 128 * b:128 * b + 128], False, b == 7)
+    need("v", p_pw)
+    c_pw = vcopy(T.PW[:], T.PWB[:, 128:256])
+    need("v", c_kp, k_key)
+    a = ts(T.TU[:], T.KEY[:], T.KP[:], OP.is_gt)
+    c_mk = ts(T.MK[:], T.J16[:, 0:64], q_, OP.is_equal)
+    need("v", a)
+    c_tri = tt(T.TRI[:], T.TU[:], T.BO[:], OP.mult)
 
-    if rank == 0:
-        c_po = vcopy(T.POFF[:, 0:1], T.QO[:])
-
-    def fold(e, lst):
-        win, c = T.IR[:], k_ir
+    def fold(e, lst, win, c):
         for i in lst:
             need(e, arrive("e1", i))
             o = T.FB[:, 128 * i:128 * i + 128]
@@ -327,121 +351,129 @@ def rank_program(g, core, T, topo):
             need(e, c)
             win = o
         return win, c
+
+    def look(out, win, by, *toks):
+        need("v", *toks)
+        return vcopy(out, win.indirect(by))
+    need("v", c_pw, k_ir)
     need("s", k_ir)
-    if rank > 0:
-        zero = T.LL[:, 0:1]
-        if first or j == 0:
-            win, c = fold("v", list(range(rank - 1, 0, -1)))
-            need("v", arrive("e1", 0))
+    if rank == 0:
+        st = vcopy(T.S0[:, 0:1], T.PW[:, 0:1])
+    else:
+        by = T.LL[:, 0:1]
+        far = list(range(mine[0] - 1, 0, -1))
+        if first:
+            win, c = fold("v", list(range(rank - 1, 0, -1)), T.PW[:], c_pw)
+            a = arrive("e1", 0)
+        elif j == 0:
+            low, c = fold("s", far[-1:], T.IR[:], k_ir)
+            win, _ = fold("v", far[:-1], T.PW[:], c_pw)
+            a = look(T.X4[:], low, by, arrive("e1", 0), c)
+            by = T.X4[:, 0:1]
         else:
-            far, c = fold("s", list(range(mine[0] - 1, 0, -1)))
-            win, _ = fold("v", list(range(rank - 1, mine[0] - 1, -1)))
-            need("v", arrive("e1", 0), c)
-            a = vcopy(T.X4[:], far.indirect(zero))
-            need("v", a)
-            zero = T.X4[:, 0:1]
-        c_po = ts(T.POFF[:], win.indirect(zero), T.QO[:], OP.add)
-    need("s", c_po, c_p, s_p)
-    st = scopy(T.JK[:], T.PW[:].indirect(T.POFF[:, 0:1]), accum_out=T.ST[:, 0:1])
-    need("v", p_tt)
-    for k in range(4):
-        need("v", st)
-        col = T.ST[:, k:k + 1]
-        if k < 3:
-            a = ts(T.TA[:, k, :], T.PTT[:, k, :], col, OP.subtract, 512.0, OP.mult)
-        for m in range(2):
-            c_of = ts(T.OFP[:, 2 * k + m:2 * k + m + 1], col, float(128 * (2 * k + m)), OP.add)
-        if k < 3:
-            need("v", a)
-            st = did("v", V.tensor_reduce(T.ST[:, k + 1:k + 2], T.TA[:, k, :], AX.X, OP.min, apply_absolute_value=True))
+            own = list(range(rank - 1, mine[0] - 1, -1))
+            few = len(own) < len(far)
+            mid, c = fold("s", far[:-1] if few else far, T.IR[:], k_ir)
+            win, _ = fold("v", own, T.PW[:], c_pw)
+            a = arrive("e1", 0)
+            if few:
+                low, _ = fold("v", far[-1:], T.IR[:], k_ir)
+                a = look(T.X1[:], low, by, a)
+                by = T.X1[:, 0:1]
+            a = look(T.X4[:], mid, by, a, c)
+            by = T.X4[:, 0:1]
+        st = look(T.S0[:], win, by, a)
+    need("s", p_e)
+    s_ew = act(T.EW[:], T.PE0[:], ACT.Relu, scale=64.0, bias=-63.0)
+    need("v", p_tt, p_ta, k_kc, st)
+    a = ts(T.TA[:, 0, :], T.PTT[:, 0, :], T.S0[:, 0:1], OP.subtract, 512.0, OP.mult)
+    b = ts(T.S1[:], T.S0[:, 0:1], T.M1[:], OP.mult)
+    need("v", a)
+    a = did("v", V.tensor_reduce(T.RA[:], T.TA[:, 0, :], AX.X, OP.min, apply_absolute_value=True))
+    need("v", a, b)
+    st = ts(T.ST[:, 0:1], T.RA[:], T.MU[:], OP.mult, T.S1[:], OP.add)
+    need("v", st)
+    a = ts(T.TA[:, 1, :], T.PTT[:, 1, :], T.ST[:, 0:1], OP.subtract, 512.0, OP.mult)
+    ts(T.OFP[:, 0:2], T.KC[:, 0:2], T.ST[:, 0:1], OP.add)
+    need("v", a)
+    st = did("v", V.tensor_reduce(T.ST[:, 1:2], T.TA[:, 1, :], AX.X, OP.min, apply_absolute_value=True))
+    need("v", st)
+    c_of = ts(T.OFP[:, 2:4], T.KC[:, 2:4], T.ST[:, 1:2], OP.add)
     need("v", c_of, s_ew, c_mk)
-    a = tt(T.GV[:], T.EW[:].indirect(T.OFP[:]), T.MK[:], OP.mult)
-    need("v", a, c_rst)
-    a = did("v", V.tensor_tensor_scan(T.SCN[:], T.RST[:], T.GV[:], 0.0, OP.mult, OP.add))
+    c_gv = tt(T.GV[:], T.EW[:].indirect(T.OFP[:]), T.MK[:], OP.mult)
+    need("v", c_gv)
+    a = ts(T.FL[:], T.GV[:], 0.0, OP.is_gt)
     need("v", a)
-    a = ts(T.FL[:], T.SCN[:, 15:128:16], 0.0, OP.is_gt)
-    need("v", a)
-    c_inc = did("v", V.tensor_tensor_scan(T.INC[:], T.ONE[:, 0:8], T.FL[:], 0.0, OP.mult, OP.add))
-    need("t", c_inc, s_tri)
-    mm(T.PSO[:, 0:1], T.TRI[:], T.INC[:, 7:8])
-    p_n = mm(T.PSO[:, 1:2], T.BO[:], T.INC[:, 7:8])
-    need("v", p_n, c_inc)
-    a = ts(T.POS[:], T.INC[:], T.PSO[:, 0:1], OP.add)
-    need("v", c_f)
-    c_n = vcopy(T.NB[:, 8 * rank:8 * rank + 1] if first else T.F[:, own + 128:own + 129], T.PSO[:, 1:2])
-    need("v", a, c_io1)
-    for i in range(8):
-        a = ts(T.OH[:, i, :], T.IO1[:], T.POS[:, i:i + 1], OP.is_equal, T.SCN[:, 16 * i + 15:16 * i + 16], OP.mult)
-        need("t", a)
-        p_a = mm(T.PSA[:, 256:320], T.BO[:], T.OH[:, i, :], i == 0, i == 7)
-    need("v", p_a)
-    c_a = ts(T.F[:, own + 48:own + 112], T.PSA[:, 256:320], -1.0, OP.add)
-    c_now = vcopy(T.NOW[:], T.PSO[:, 1:2])
-
-    def part(x, lo, hi):
-        return T.F[:, SL * x + lo:SL * x + hi]
-    wide = 128 if first else SL
-
-    def slot_f(d):
-        return part(1 + j if d in mine else (0 if d > rank else 1 + len(mine)), 0, wide)
-    if first:
-        need("q", c_n)
-        send("en", later(rank), T.NB[:, 8 * rank:8 * rank + 8], lambda d: T.NB[:, 8 * rank:8 * rank + 8])
-    need("q", c_a, c_n)
-    send("ev", e2(rank), part(1 + j, 0, wide), slot_f)
-
-    for i in range(rank):
-        if same(i, 0):
-            need("v", arrive("en", i))
-    if not first:
-        c_4 = did("v", V.tensor_reduce(T.C4[:], T.NB[:, 0:8 * mine[0] - 7:8], AX.X, OP.add))
-    for i in range(rank):
-        if rank in e2(i):
-            need("v", arrive("ev", i))
-    beg = 0.0
-    if rank > 0:
-        c_np = vcopy(T.NPV[:], T.NB[:, 8 * rank - 8:8 * rank - 7] if first or j == 0 else part(j, 128, 129))
-    if j > 1:
-        a = did("v", V.tensor_reduce(T.BG0[:], T.NB[:, 0:8 * j - 7:8] if first
-                                     else T.F[:, SL + 128:SL + 129 + SL * (j - 1):SL], AX.X, OP.add))
-    if rank > 0:
-        need("v", c_np)
-    if j == 1:
-        beg = T.NPV[:]
-    elif j > 1:
-        need("v", a)
-        beg = T.BG0[:]
-    if not first:
-        need("v", c_4)
-        if j == 0:
-            beg = T.C4[:]
-        else:
-            a = tt(T.BG[:], T.C4[:], beg, OP.add)
-            need("v", a)
-            beg = T.BG[:]
-    need("v", c_qi, c_a, c_n, c_now)
-    for i, (x, what) in enumerate(lists):
-        o, q2 = T.OF2[:, 2 * i:2 * i + 2], T.QI[:, 2 * i:2 * i + 2]
-        if what == "own":
-            a = ts(o, q2, beg, OP.subtract)
-        elif what == "prev":
-            a = ts(o, q2, beg, OP.subtract, T.NPV[:], OP.add)
-        else:
-            a = ts(o, q2, beg, OP.subtract, T.NOW[:], OP.subtract)
-    n = len(lists)
-    need("v", a)
+    c_inc = scan(T.INC[:], T.ONE[:, 0:64], T.FL[:], OP.mult, OP.add)
+    need("t", c_inc, c_tri, s_w3, c_wh)
+    p_b = mm(T.PSO[:, 0:1], T.TRI[:], T.INC[:, 63:64])
+    p_n = mm(T.PWA[:, 0:1], T.BO[:], T.INC[:, 63:64])
+    need("v", k_rst)
+    c_scn = scan(T.SCN[:], T.RST[:], T.GV[:], OP.mult, OP.add)
+    need("v", p_b, c_inc)
+    c_pos = ts(T.POS[:], T.INC[:, 15:64:16], T.PSO[:, 0:1], OP.add)
+    need("s", p_n, k_nb)
+    s_n = scopy(T.NB[:, 8 * rank:8 * rank + 1], T.PWA[:, 0:1])
     if rank + 1 < NR:
-        need("v", arrive("ev", rank + 1))
-    a = vcopy(T.YG[:, 0:32 * n], T.F[:, SL * w0:SL * w1 + 128].indirect(T.OF2[:, 0:2 * n]))
+        need("q", s_n)
+        send("en", later(rank), T.NB[:, 8 * rank:8 * rank + 8], lambda d: T.NB[:, 8 * rank:8 * rank + 8])
+    need("s", c_scn)
+    s_nv = scopy(T.NV[:], T.SCN[:, 15:64:16], scale=-1.0)
+    need("s", c_pos, k_io1)
+    a = act(T.OD[:], T.IO1[:], ACT.Abs, scale=-1.0, bias=T.POS[:, 3:4])
+    need("s", a, s_nv)
+    s_oh = act(T.OH[:, 3, :], T.OD[:], ACT.Relu, scale=T.NV[:, 3:4], bias=T.SCN[:, 63:64])
+    s_own = scopy(T.OWN[:], T.PWA[:, 0:1])
+    need("v", c_pos, c_scn, k_io1)
+    for i in range(4):
+        if i < 3:
+            a = ts(T.OH[:, i, :], T.IO1[:], T.POS[:, i:i + 1], OP.is_equal, T.SCN[:, 16 * i + 15:16 * i + 16], OP.mult)
+        need("t", a if i < 3 else s_oh)
+        p_a = mm(T.PSA[:, 256:320], T.BO[:], T.OH[:, i, :], i == 0, i == 3)
+    a = c_qi = ts(T.QI[:], T.IR[:, 0:17:16], q_, OP.add, float(32 * rank), OP.add)
+    need("v", p_a)
+    c_a = ts(T.F[:, 64:128], T.PSA[:, 256:320], -1.0, OP.add)
+    need("q", c_a)
+    n = 64 if rank + 1 < NR else 16
+    send("ev", beside(rank), T.F[:, 64:64 + n], lambda d: T.F[:, 0:n] if d > rank else T.F[:, 128:128 + n])
+
+    lo = 0 if rank > 0 else 64
+    hi = 192 if rank + 2 < NR else 144 if rank + 1 < NR else 128
+    u = T.QI[:]
+    need("v", s_own)
+    c_b1 = ts(T.B1[:], T.OWN[:], -1.0, OP.mult, 64.0, OP.add)
+    if rank > 0:
+        for i in range(rank):
+            need("v", arrive("en", i))
+        b = did("v", V.tensor_reduce(T.BEG[:], T.NB[:, 0:8 * rank - 7:8], AX.X, OP.add))
+        c_a1 = ts(T.A1[:], T.NB[:, 8 * rank - 8:8 * rank - 7], 64.0, OP.subtract)
+        need("v", b, c_qi)
+        u = T.U[:]
+        a = ts(u, T.QI[:], T.BEG[:], OP.subtract)
     need("v", a)
-    out = T.Y1
-    a = tt(T.Y1[:], T.YG[:, 0:32], T.YG[:, 32:64], OP.max)
-    if n == 3:
-        need("v", a)
-        out = T.Y2
-        a = tt(T.Y2[:], T.Y1[:], T.YG[:, 64:96], OP.max)
+    o = u
+    if rank + 1 < NR:
+        need("v", c_b1)
+        b = ts(T.U1[:], u, T.OWN[:], OP.is_ge, T.B1[:], OP.mult)
+    if rank > 0:
+        need("v", c_a1)
+        c = ts(T.U3[:], u, 0.0, OP.is_lt, T.A1[:], OP.mult)
+    if rank + 1 < NR:
+        need("v", b)
+        o = T.U2[:]
+        a = tt(o, u, T.U1[:], OP.add)
+    if rank > 0:
+        need("v", a, c)
+        a = tt(T.U4[:], o, T.U3[:], OP.add)
+        o = T.U4[:]
+    need("v", a)
+    a = ts(T.OF2[:], o, float(64 - lo), OP.add)
+    for i in beside(rank):
+        need("v", arrive("ev", i))
+    need("v", a, c_a)
+    a = vcopy(T.Y1[:], T.F[:, lo:hi].indirect(T.OF2[:]))
     need("y", a)
-    g.sync.dma_start(T.y[:, :], out[0:128:16, :]).then_inc(T.sem.dy, 16)
+    g.sync.dma_start(T.y[:, :], T.Y1[0:128:16, :]).then_inc(T.sem.dy, 16)
     need("y", ("dy", 16))
     for e in ("v", "s", "t", "q"):
         need("q", (e, cnt[e]))

from concourse.bass import DstId, RemoteDMATransfer
from concourse.mybir import dt, AluOpType, AxisListType, ActivationFunctionType

_BUF = {
    "int32": "PI:1 CI:4 SYI:2x32 X:2x128 XA:2x128 EM:2x128 EI0:2x128",
    "uint16": "LST:3x64 LA:32 LB:16 LC:8 LL:64 X1:16 X4:16 OFP:4 OF2:2",
    "float32": "PF:1 CF:4 RI:128 IR:128 GC:128 J16:128 KEY:128 MG:4 MS:16 S0:16 Q1:1 CORR:1 MU:1 M1:1 K1:1 KP:1 RA:1 S1:1 "
               "SD0:128 SD1:128 KC:4 EMF:2x128 EA:2x128 QI:2 ST:2 TA:2x128 NV:4 OWN:1 BEG:1 A1:1 B1:1 U:2 U1:2 U2:2 U3:2 "
               "U4:2 Y1:32",
    "bfloat16": "R:128 XR:128 BRR:192 DG:8x128 ZB:128 G4:128 R3:128 BO:128 RB:8x128 ONE:128 IO1:64 TU:128 TRI:128 "
                "SYB:2x32 XT:2x128 XS:2x128 XB:2x128 EB:2x2x128 SG:2x2x128 SEL:4x2x8 LS:4x2x64 LSH:2x2x64 YB:16x64 T3:128 "
                "T1:128 WH:1024 HH:1024 W3:1024 W2:1024 W1:1024 W0:1024 QM:512 HM:256 MM:128 SD:128 SCA:512 SCB:256 "
                "SCC:128 SCM:128 FB:896 M6:128 PW:128 EW:512 MK:64 RST:64 GV:64 SCN:64 FL:64 INC:64 POS:4 OH:4x64 OD:64 "
                "NB:64 F:192",
}
SCRATCH = {n: ("sbuf", [128] + [int(x) for x in d.split("x")], t)
           for t, l in _BUF.items() for n, d in (w.split(":") for w in l.split())}
for _n, _d in (("PSA", [512]), ("PSL", [64, 8]), ("PWA", [512]), ("PWB", [512]), ("PTT", [4, 128]), ("PE0", [512]),
               ("PE1", [512]), ("PSO", [512])):
    SCRATCH[_n] = ("psum", [128] + _d, "float32")
SEMAPHORES = (["v", "s", "t", "q", "dsy", "dx", "dxs", "dem", "dy", "ls"]
              + [p + "_%d" % j for p in ("e1", "en", "ev") for j in range(8)])


def rank_program(g, core, T, topo):
    rank = T.rank_of(core)
    if rank is None:
        return
    OP, ACT, AX = AluOpType, ActivationFunctionType, AxisListType
    NR = len(T.cores)
    mine = [r for r, c in enumerate(T.cores) if topo.chip(c) == topo.chip(core)]
    j = mine.index(rank)
    first = mine[0] == 0
    Q = {"v": g.vector, "s": g.scalar, "t": g.tensor, "q": g, "y": g.sync}
    cnt = {"v": 0, "s": 0, "t": 0, "q": 0}
    seen = {}
    V, S, PE = g.vector, g.scalar, g.tensor

    def need(e, *toks):
        for sem, n in toks:
            if seen.get((e, sem), 0) < n:
                Q[e].wait_ge(T.sem[sem], n)
                seen[(e, sem)] = n

    def did(e, ins):
        cnt[e] += 1
        ins.then_inc(T.sem[e], 1)
        return (e, cnt[e])

    def ts(out, in0, s1, op0, s2=None, op1=None):
        if op1 is None:
            return did("v", V.tensor_scalar(out, in0, s1, None, op0))
        return did("v", V.tensor_scalar(out, in0, s1, s2, op0, op1))

    def tt(out, in0, in1, op):
        return did("v", V.tensor_tensor(out, in0, in1, op))

    def vcopy(out, in_):
        return did("v", V.tensor_copy(out, in_))

    def fill(ap, x):
        return did("v", V.memset(ap, x))

    def scan(out, d0, d1, o0, o1):
        return did("v", V.tensor_tensor_scan(out, d0, d1, 0.0, o0, o1))

    def act(out, in_, func, **k):
        return did("s", S.activation(out, in_, func, **k))

    def scopy(out, in_, **k):
        return act(out, in_, ACT.Copy, **k)

    def mm(out, lhsT, rhs, start=True, stop=True):
        return did("t", PE.matmul(out, lhsT, rhs, start, stop))

    def iota(out, pattern, cm=0, base=0):
        return did("q", g.iota(out, pattern, base, cm, allow_small_or_imprecise_dtypes=True))

    def same(r, r2):
        return topo.chip(T.cores[r]) == topo.chip(T.cores[r2])

    def plan(r, dsts):
        near, far = [d for d in dsts if same(r, d)], [d for d in dsts if not same(r, d)]
        p = []
        if near:
            es = topo.engines(T.cores[r], T.cores[near[0]])
            if far or r + 1 == NR:
                other = [d for d in range(NR) if not same(r, d)][0]
                es = [e for e in es if e not in topo.engines(T.cores[r], T.cores[other])]
            p.append((near, es))
        if far:
            p.append((far, topo.engines(T.cores[r], T.cores[far[0]])))
        return p

    def later(r):
        return list(range(NR - 1, r, -1))

    def beside(r):
        return [x for x in range(NR) if abs(x - r) == 1]

    def arrive(kind, r):
        dsts = beside(r) if kind == "ev" else later(r)
        return ("%s_%d" % (kind, r), [len(es) for ds, es in plan(r, dsts) if rank in ds][0])
    sent = [0]

    def send(kind, dsts, src_, where):
        trs = []
        for ds, es in plan(rank, dsts):
            adr = [topo.addr(T.cores[d]) for d in ds]
            trs.append(RemoteDMATransfer(dst_ids=[DstId(rid=x[0], pnc=x[1]) for x in adr],
                                         dma_engine_mask=sum(1 << e for e in es),
                                         remote_sem=T.sem["%s_%d" % (kind, rank)], srcs=[src_], dsts=[where(d) for d in ds]))
            sent[0] += len(es)
        g.remote_dma_fused(trs, local_sem=T.sem.ls)

    g.sync.dma_start(T.X[:, 0, :], T.nx[0:4, :]).then_inc(T.sem.dx, 16)
    S.dma_start(T.X[:, 1, :], T.nx[4:8, :]).then_inc(T.sem.dxs, 16)
    g.sync.dma_start(T.SYI[0:4, 0, :], T.sy[0:4, :]).then_inc(T.sem.dsy, 16)
    S.dma_start(T.SYI[0:4, 1, :], T.sy[4:8, :]).then_inc(T.sem.dsy, 16)
    g.sync.dma_start(T.EM[:, 0, :], T.em[0:4, :]).then_inc(T.sem.dem, 16)
    g.sync.dma_start(T.EM[:, 1, :], T.em[4:8, :]).then_inc(T.sem.dem, 16)
    dsy, dx, dxs, dem = ("dsy", 32), ("dx", 16), ("dxs", 16), ("dem", 32)

    k_pi = did("q", g.iota(T.PI[:], [[0, 1]], 0, 1))
    k_gc = iota(T.GC[:], [[1, 8], [0, 16]])
    k_ir = iota(T.IR[:], [[1, 128]])
    k_ri = iota(T.RI[0:4, :], [[1, 4], [0, 32]])
    k_pf = iota(T.PF[:], [[0, 1]], 1)
    k_j16 = iota(T.J16[:], [[0, 8], [1, 16]])
    k_br = iota(T.BRR[0:1, :], [[0, 6], [128, 4], [0, 8]])
    k_xr = iota(T.XR[:], [[1, 128]])
    k_key = iota(T.KEY[:], [[0, 8], [1, 2], [2, 8]])
    k_kc = iota(T.KC[:], [[128, 4]])

    c_ls0 = fill(T.LS[:], 0.0)
    need("v", k_pi)
    for i, (x, op) in enumerate(((15, OP.bitwise_and), (31, OP.bitwise_and), (5, OP.arith_shift_right),
                                 (4, OP.arith_shift_right))):
        a = ts(T.CI[:, i:i + 1], T.PI[:], x, op)
    need("v", a)
    c_cf = vcopy(T.CF[:], T.CI[:])
    q_, a_, gt_, gp_ = [T.CF[:, i:i + 1] for i in range(4)]
    need("v", c_cf, k_gc)
    c_bo = ts(T.BO[:], T.GC[:], gp_, OP.is_equal)
    c_mu = ts(T.MU[:], q_, 8.0, OP.is_ge)
    ts(T.M1[:], q_, 8.0, OP.is_lt)
    need("v", k_ir)
    c_ms = ts(T.MS[:], T.IR[:, 0:16], q_, OP.is_equal)
    c_mg = ts(T.MG[:], T.IR[:, 0:4], gt_, OP.is_equal)
    c_one = fill(T.ONE[:], 1.0)
    need("v", c_mu)
    c_k1 = ts(T.K1[:], T.MU[:], -15.0, OP.mult)
    need("s", c_bo, c_ms)
    for b in range(8):
        s_rb = scopy(T.RB[:, b, :], T.BO[:], scale=T.MS[:, b:b + 1])
    need("v", c_k1)
    c_kp = ts(T.KP[:], q_, 2.0, OP.mult, T.K1[:], OP.add)
    need("v", k_ri, k_pf)
    c_r = ts(T.R[0:4, :], T.RI[0:4, :], T.PF[0:4, :], OP.is_equal)
    need("v", dsy)
    c_syb = vcopy(T.SYB[0:4], T.SYI[0:4])
    need("t", c_syb, c_r)
    for k in range(4):
        p_rep = mm(T.PSA[:, 16 * k:16 * k + 16], T.R[0:4, :], T.SYB[0:4, :, k:32:4])
    need("v", dx, dxs)
    a = ts(T.XA[:], T.X[:], 127, OP.bitwise_and)
    need("v", p_rep)
    c_sel = ts(T.SEL[:], T.PSA[:, 0:64], a_, OP.is_equal)
    need("v", a)
    c_xt = vcopy(T.XT[:], T.XA[:])
    need("s", c_sel, c_mg, c_ls0)
    for gg in range(4):
        s_ls = scopy(T.LS[:, :, :, 16 * gg:16 * gg + 8], T.SEL[:], scale=T.MG[:, gg:gg + 1])
    need("t", s_ls, c_xt)
    for t in range(2):
        p_t3 = mm(T.PSA[64 * t:64 * t + 64, 128:256], T.LS[:, 3, t, :], T.XT[:, t, :])
    need("s", p_t3)
    s_t3 = scopy(T.T3[:], T.PSA[:, 128:256])
    need("v", c_xt, c_mg)
    c_yb = []
    for t in range(2):
        for gg in range(4):
            a = ts(T.YB[:, 8 * t:8 * t + 8, 16 * gg:16 * gg + 16], T.XT[:, t, :], T.MG[:, gg:gg + 1], OP.mult)
        c_yb.append(a)

    def lists(t):
        need("t", c_one, k_br)
        mm(T.PSL[64 * t:64 * t + 64, 0:24, :], T.ONE[0:1, 0:64], T.BRR[0:1, :], True, False)
        need("t", c_yb[t], c_sel)
        for c in range(8):
            x = mm(T.PSL[64 * t:64 * t + 64, 0:24, c], T.YB[:, 8 * t + c, :], T.SEL[:, 0:3, t, :], False, c == 7)
        return x
    lists(0)
    need("t", s_t3, s_rb)
    for b in range(4):
        p_wb = mm(T.PWB[:, 128 * b:128 * b + 128], T.RB[:, 4 + b, :], T.T3[:])
    for b in range(3):
        p_wa = mm(T.PWA[:, 128 * b:128 * b + 128], T.RB[:, b, :], T.T3[:])
    p_w3 = mm(T.PSO[:, 0:128], T.RB[:, 3, :], T.T3[:])
    p_l = lists(1)
    for t in range(2):
        p_t1 = mm(T.PSA[64 * t:64 * t + 64, 320:448], T.LS[:, 1, t, :], T.XT[:, t, :])
    need("s", p_wb)
    s_w = scopy(T.W3[:, 512:1024], T.PWB[:])
    need("s", p_w3)
    s_w3 = scopy(T.W3[:, 384:512], T.PSO[:, 0:128])
    need("s", p_t1)
    s_t1 = scopy(T.T1[:], T.PSA[:, 320:448])
    need("v", k_j16)
    a = ts(T.Q1[:], q_, 1.0, OP.add)
    x0 = ts(T.SD0[:], T.J16[:], q_, OP.is_equal, -65536.0, OP.mult)
    need("v", a)
    x1 = ts(T.SD1[:], T.J16[:], T.Q1[:], OP.is_equal, 128.0, OP.mult)
    ts(T.CORR[:], q_, 15.0, OP.is_lt, -128.0, OP.mult)
    need("v", x0, x1)
    c_sd = tt(T.SD[:], T.SD0[:], T.SD1[:], OP.add)
    need("v", p_wa)
    c_w = vcopy(T.W3[:, 0:384], T.PWA[:, 0:384])
    need("v", p_l)
    c_l = vcopy(T.LST[:], T.PSL[:, 0:24, :])
    need("t", s_t1, s_w, c_w)
    for b in range(8):
        p_wh = mm((T.PE1 if b > 3 else T.PWA)[:, 128 * (b % 4):128 * (b % 4) + 128], T.RB[:, b, :], T.T1[:])

    need("q", c_bo, c_one, s_rb)
    for b in (5, 6, 7, 4, 0, 1, 2, 3):
        k_dg = did("q", g.affine_select(T.DG[:, b, :], T.RB[:, b, :], [[0, 8], [0, 2], [1, 8]], OP.is_equal, 0.0, -b, 0))
    k_rst = did("q", g.affine_select(T.RST[:], T.ONE[:, 0:64], [[0, 4], [1, 16]], OP.not_equal, 0.0, 0, 0))
    k_io1 = iota(T.IO1[:], [[1, 64]], 0, 1)
    k_nb = iota(T.NB[:, 8 * rank:8 * rank + 8], [[0, 8]])

    src = T.W3
    need("v", s_w3)
    for k, dst in ((2, T.W2), (1, T.W1), (0, T.W0)):
        need("v", c_w, c_l)
        need("s", s_w, c_l)
        c_w = vcopy(dst[:, 0:512], src[:, 0:512].indirect(T.LST[:, k, 0:32]))
        s_w = scopy(dst[:, 512:1024], src[:, 512:1024].indirect(T.LST[:, k, 32:64]))
        src = dst

    def to_lists(lst, sc, win, slots, at=0):
        for i, s in enumerate(slots):
            x = scan(sc[:, 128 * (at + i):128 * (at + i) + 128], T.SD[:], win[:, 128 * s:128 * s + 128], OP.add, OP.max)
        need("v", x)
        n = len(slots)
        return ts(lst[:, 8 * at:8 * at + 8 * n], sc[:, 128 * at + 15:128 * (at + n):16], T.CORR[:], OP.add)

    def w0(b):
        return T.W0[:, 128 * b:128 * b + 128]

    def qm(b):
        return T.QM[:, 128 * b:128 * b + 128]
    need("v", c_w, s_w, c_sd)
    l1 = to_lists(T.LA, T.SCA, T.W0, [4, 6], 2)
    l0 = to_lists(T.LA, T.SCA, T.W0, [0, 2])
    need("v", l0)
    c_q = vcopy(qm(0), w0(1).indirect(T.LA[:, 0:8]))
    need("s", l1)
    s_q2 = scopy(qm(2), w0(5).indirect(T.LA[:, 16:24]))
    s_q = scopy(qm(3), w0(7).indirect(T.LA[:, 24:32]))
    need("s", l0)
    s_q1 = scopy(qm(1), w0(3).indirect(T.LA[:, 8:16]))
    need("v", c_q, s_q2)
    c_lb = to_lists(T.LB, T.SCB, T.QM, [0, 2])
    need("v", c_lb, s_q1)
    c_h = vcopy(T.HM[:, 0:128], qm(1).indirect(T.LB[:, 0:8]))
    need("s", c_lb, s_q1)
    s_h = scopy(T.HM[:, 128:256], qm(3).indirect(T.LB[:, 8:16]))
    need("v", c_h)
    c_lc = to_lists(T.LC, T.SCC, T.HM, [0])
    need("v", c_lc, s_h)

    def slot_l(r):
        return T.LL[:, 8 * r:8 * r + 8]
    if rank + 1 < NR:
        c_m = vcopy(T.MM[:], T.HM[:, 128:256].indirect(T.LC[:]))
        need("v", c_m)
        c_lm = to_lists(slot_l(rank), T.SCM, T.MM, [0])
        need("q", c_lm)
        send("e1", later(rank), slot_l(rank), lambda d: slot_l(rank))

    s_m6 = scopy(T.M6[:], w0(6).indirect(T.LB[:, 8:16]))
    s_r3 = scopy(T.R3[:], w0(2).indirect(T.LB[:, 0:8]))

    def choose(out, what):
        for i, (b, win) in enumerate(what):
            x = mm(out, T.DG[:, b, :], win, i == 0, i + 1 == len(what))
        return x
    need("t", s_m6, c_h, k_dg, k_xr, s_w, c_lc)
    p_z = choose(T.PWB[:, 0:128], [(4, T.XR[:]), (5, w0(4)), (6, qm(2)), (7, T.M6[:])])
    need("v", p_wh)
    c_wh = vcopy(T.WH[:, 0:512], T.PWA[:])
    need("s", p_wh)
    s_wh = scopy(T.WH[:, 512:1024], T.PE1[:])
    need("s", p_z)
    s_z = scopy(T.ZB[:], T.PWB[:, 0:128])
    need("s", c_xt, c_sel, c_mg)
    s_xs = scopy(T.XS[:], T.XT[:], scale=1.0 / 512.0)
    for gg in range(4):
        for u in range(2):
            s_lh = scopy(T.LSH[:, :, :, 16 * gg + 8 * u:16 * gg + 8 * u + 8], T.SEL[:, 2 * u:2 * u + 2], scale=T.MG[:, gg:gg + 1])
    c_xb = vcopy(T.XB[:], T.X[:])
    need("v", s_z)
    c_g4 = vcopy(T.G4[:], T.ZB[:].indirect(T.LC[:]))
    need("t", s_xs, k_xr, c_one, s_lh)
    for t in range(2):
        mm(T.PTT[64 * t:64 * t + 64, 1, :], T.ONE[0:1, 0:64], T.XR[0:1, :], True, False)
        p_tt = mm(T.PTT[64 * t:64 * t + 64, 1, :], T.LSH[:, 0, t, :], T.XS[:, t, :], False, True)
    need("t", c_g4, s_r3)
    p_pw = choose(T.PWB[:, 128:256], [(0, T.XR[:]), (1, w0(0)), (2, qm(0)), (3, T.R3[:])]
                  + [(b, T.G4[:]) for b in (4, 5, 6, 7)])
    need("v", dem)
    c_em = ts(T.EMF[:], T.EM[:], -31.5, OP.add)
    a = ts(T.EI0[:], T.EM[:], 63, OP.bitwise_and)
    need("s", c_xb)
    act(T.SG[:, :, 0, :], T.XB[:], ACT.Sign, bias=-127.5)
    act(T.SG[:, :, 1, :], T.XB[:], ACT.Sign, bias=-255.5)
    need("v", a)
    c_eb = ts(T.EB[:, :, 0, :], T.EI0[:], 1.0 / 64.0, OP.mult)
    need("s", c_em)
    a = scopy(T.EA[:], T.EMF[:], scale=1.0 / 64.0, bias=12582912.0)
    need("s", a)
    s_eb = scopy(T.EB[:, :, 1, :], T.EA[:], scale=1.0 / 64.0, bias=-196608.0)
    need("t", c_eb, s_eb)
    for k in range(2):
        for t in range(2):
            o = T.PE0[64 * t:64 * t + 64, 256 * k:256 * k + 256]
            mm(o, T.LSH[:, k, t, :], T.SG[:, t], True, False)
            p_e = mm(o, T.LSH[:, k, t, :], T.EB[:, t], False, True)
    need("v", c_wh)
    c_hh = ts(T.HH[:, 0:512], T.WH[:, 0:512].indirect(T.LST[:, 0, 0:32]), 1.0 / 512.0, OP.mult)
    need("s", s_wh)
    s_hh = scopy(T.HH[:, 512:1024], T.WH[:, 512:1024].indirect(T.LST[:, 0, 32:64]), scale=1.0 / 512.0)
    need("t", c_hh, s_hh)
    mm(T.PTT[:, 0, :], T.ONE[0:1, :], T.XR[0:1, :], True, False)
    for b in range(8):
        p_ta = mm(T.PTT[:, 0, :], T.DG[:, b, :], T.HH[:, 128 * b:128 * b + 128], False, b == 7)
    need("v", p_pw)
    c_pw = vcopy(T.PW[:], T.PWB[:, 128:256])
    need("v", c_kp, k_key)
    a = ts(T.TU[:], T.KEY[:], T.KP[:], OP.is_gt)
    c_mk = ts(T.MK[:], T.J16[:, 0:64], q_, OP.is_equal)
    need("v", a)
    c_tri = tt(T.TRI[:], T.TU[:], T.BO[:], OP.mult)

    def fold(e, lst, win, c):
        for i in lst:
            need(e, arrive("e1", i))
            o = T.FB[:, 128 * i:128 * i + 128]
            c = (vcopy if e == "v" else scopy)(o, win.indirect(slot_l(i)))
            need(e, c)
            win = o
        return win, c

    def look(out, win, by, *toks):
        need("v", *toks)
        return vcopy(out, win.indirect(by))
    need("v", c_pw, k_ir)
    need("s", k_ir)
    if rank == 0:
        st = vcopy(T.S0[:, 0:1], T.PW[:, 0:1])
    else:
        by = T.LL[:, 0:1]
        far = list(range(mine[0] - 1, 0, -1))
        if first:
            win, c = fold("v", list(range(rank - 1, 0, -1)), T.PW[:], c_pw)
            a = arrive("e1", 0)
        elif j == 0:
            low, c = fold("s", far[-1:], T.IR[:], k_ir)
            win, _ = fold("v", far[:-1], T.PW[:], c_pw)
            a = look(T.X4[:], low, by, arrive("e1", 0), c)
            by = T.X4[:, 0:1]
        else:
            own = list(range(rank - 1, mine[0] - 1, -1))
            few = len(own) < len(far)
            mid, c = fold("s", far[:-1] if few else far, T.IR[:], k_ir)
            win, _ = fold("v", own, T.PW[:], c_pw)
            a = arrive("e1", 0)
            if few:
                low, _ = fold("v", far[-1:], T.IR[:], k_ir)
                a = look(T.X1[:], low, by, a)
                by = T.X1[:, 0:1]
            a = look(T.X4[:], mid, by, a, c)
            by = T.X4[:, 0:1]
        st = look(T.S0[:], win, by, a)
    need("s", p_e)
    s_ew = act(T.EW[:], T.PE0[:], ACT.Relu, scale=64.0, bias=-63.0)
    need("v", p_tt, p_ta, k_kc, st)
    a = ts(T.TA[:, 0, :], T.PTT[:, 0, :], T.S0[:, 0:1], OP.subtract, 512.0, OP.mult)
    b = ts(T.S1[:], T.S0[:, 0:1], T.M1[:], OP.mult)
    need("v", a)
    a = did("v", V.tensor_reduce(T.RA[:], T.TA[:, 0, :], AX.X, OP.min, apply_absolute_value=True))
    need("v", a, b)
    st = ts(T.ST[:, 0:1], T.RA[:], T.MU[:], OP.mult, T.S1[:], OP.add)
    need("v", st)
    a = ts(T.TA[:, 1, :], T.PTT[:, 1, :], T.ST[:, 0:1], OP.subtract, 512.0, OP.mult)
    ts(T.OFP[:, 0:2], T.KC[:, 0:2], T.ST[:, 0:1], OP.add)
    need("v", a)
    st = did("v", V.tensor_reduce(T.ST[:, 1:2], T.TA[:, 1, :], AX.X, OP.min, apply_absolute_value=True))
    need("v", st)
    c_of = ts(T.OFP[:, 2:4], T.KC[:, 2:4], T.ST[:, 1:2], OP.add)
    need("v", c_of, s_ew, c_mk)
    c_gv = tt(T.GV[:], T.EW[:].indirect(T.OFP[:]), T.MK[:], OP.mult)
    need("v", c_gv)
    a = ts(T.FL[:], T.GV[:], 0.0, OP.is_gt)
    need("v", a)
    c_inc = scan(T.INC[:], T.ONE[:, 0:64], T.FL[:], OP.mult, OP.add)
    need("t", c_inc, c_tri, s_w3, c_wh)
    p_b = mm(T.PSO[:, 0:1], T.TRI[:], T.INC[:, 63:64])
    p_n = mm(T.PWA[:, 0:1], T.BO[:], T.INC[:, 63:64])
    need("v", k_rst)
    c_scn = scan(T.SCN[:], T.RST[:], T.GV[:], OP.mult, OP.add)
    need("v", p_b, c_inc)
    c_pos = ts(T.POS[:], T.INC[:, 15:64:16], T.PSO[:, 0:1], OP.add)
    need("s", p_n, k_nb)
    s_n = scopy(T.NB[:, 8 * rank:8 * rank + 1], T.PWA[:, 0:1])
    if rank + 1 < NR:
        need("q", s_n)
        send("en", later(rank), T.NB[:, 8 * rank:8 * rank + 8], lambda d: T.NB[:, 8 * rank:8 * rank + 8])
    need("s", c_scn)
    s_nv = scopy(T.NV[:], T.SCN[:, 15:64:16], scale=-1.0)
    need("s", c_pos, k_io1)
    a = act(T.OD[:], T.IO1[:], ACT.Abs, scale=-1.0, bias=T.POS[:, 3:4])
    need("s", a, s_nv)
    s_oh = act(T.OH[:, 3, :], T.OD[:], ACT.Relu, scale=T.NV[:, 3:4], bias=T.SCN[:, 63:64])
    s_own = scopy(T.OWN[:], T.PWA[:, 0:1])
    need("v", c_pos, c_scn, k_io1)
    for i in range(4):
        if i < 3:
            a = ts(T.OH[:, i, :], T.IO1[:], T.POS[:, i:i + 1], OP.is_equal, T.SCN[:, 16 * i + 15:16 * i + 16], OP.mult)
        need("t", a if i < 3 else s_oh)
        p_a = mm(T.PSA[:, 256:320], T.BO[:], T.OH[:, i, :], i == 0, i == 3)
    a = c_qi = ts(T.QI[:], T.IR[:, 0:17:16], q_, OP.add, float(32 * rank), OP.add)
    need("v", p_a)
    c_a = ts(T.F[:, 64:128], T.PSA[:, 256:320], -1.0, OP.add)
    need("q", c_a)
    n = 64 if rank + 1 < NR else 16
    send("ev", beside(rank), T.F[:, 64:64 + n], lambda d: T.F[:, 0:n] if d > rank else T.F[:, 128:128 + n])

    lo = 0 if rank > 0 else 64
    hi = 192 if rank + 2 < NR else 144 if rank + 1 < NR else 128
    u = T.QI[:]
    need("v", s_own)
    c_b1 = ts(T.B1[:], T.OWN[:], -1.0, OP.mult, 64.0, OP.add)
    if rank > 0:
        for i in range(rank):
            need("v", arrive("en", i))
        b = did("v", V.tensor_reduce(T.BEG[:], T.NB[:, 0:8 * rank - 7:8], AX.X, OP.add))
        c_a1 = ts(T.A1[:], T.NB[:, 8 * rank - 8:8 * rank - 7], 64.0, OP.subtract)
        need("v", b, c_qi)
        u = T.U[:]
        a = ts(u, T.QI[:], T.BEG[:], OP.subtract)
    need("v", a)
    o = u
    if rank + 1 < NR:
        need("v", c_b1)
        b = ts(T.U1[:], u, T.OWN[:], OP.is_ge, T.B1[:], OP.mult)
    if rank > 0:
        need("v", c_a1)
        c = ts(T.U3[:], u, 0.0, OP.is_lt, T.A1[:], OP.mult)
    if rank + 1 < NR:
        need("v", b)
        o = T.U2[:]
        a = tt(o, u, T.U1[:], OP.add)
    if rank > 0:
        need("v", a, c)
        a = tt(T.U4[:], o, T.U3[:], OP.add)
        o = T.U4[:]
    need("v", a)
    a = ts(T.OF2[:], o, float(64 - lo), OP.add)
    for i in beside(rank):
        need("v", arrive("ev", i))
    need("v", a, c_a)
    a = vcopy(T.Y1[:], T.F[:, lo:hi].indirect(T.OF2[:]))
    need("y", a)
    g.sync.dma_start(T.y[:, :], T.Y1[0:128:16, :]).then_inc(T.sem.dy, 16)
    need("y", ("dy", 16))
    for e in ("v", "s", "t", "q"):
        need("q", (e, cnt[e]))
    need("q", ("ls", sent[0]))
